import numpy as np
import ml_dtypes


def mxq(x, axis, fmt="e4m3"):
    dtype, down = {"e4m3": (ml_dtypes.float8_e4m3fn, 7), "e5m2": (ml_dtypes.float8_e5m2, 14)}[fmt]
    v = np.moveaxis(np.asarray(x, np.float32).astype(ml_dtypes.bfloat16).astype(np.float64), axis, -1)
    blocks = v.reshape(v.shape[:-1] + (-1, 32))
    amax = np.abs(blocks).max(-1, keepdims=True)
    byte = np.maximum(np.where(amax > 0, np.frexp(amax)[1] - 1 + 127, 0) - down, 1)
    scale = np.exp2(byte - 127.0)
    codes = (blocks / scale).astype(np.float32).astype(dtype).astype(np.float64)
    return np.moveaxis((codes * scale).reshape(v.shape), -1, axis)


WIDE = False


def mx_kscale(k):
    if not WIDE:
        return np.ones(k)
    levels = np.array([10, -10, 5, -5, 0])
    if k % 512:
        return np.exp2(np.random.permutation(np.resize(levels, k // 32))).repeat(32)
    a = np.empty((k // 512, 16))
    for p in range(k // 512):
        a[p, :8] = np.random.permutation(np.resize(levels, 8))
        for g in range(8):
            far = levels[np.abs(levels - a[p, g]) >= 10]
            a[p, g + 8] = far[np.random.randint(len(far))]
    return np.exp2(a.ravel()).repeat(32)


def f64(x):
    return np.asarray(x).astype(np.float64)


def striped(idx):
    return np.tile(idx.reshape(-1, 16).T, (8, 1)).astype(np.uint16)


def unstriped(offs):
    return offs[:16].T.reshape(-1).astype(np.int64)


E2M1 = np.array([0.0, 0.5, 1.0, 1.5, 2.0, 3.0, 4.0, 6.0, -0.0, -0.5, -1.0, -1.5, -2.0, -3.0, -4.0, -6.0])


def pack_weight(w, fmt):
    k, n = w.shape
    w = f64(np.asarray(w, np.float32).astype(ml_dtypes.bfloat16)).reshape(k // 32, 32, n)
    amax = np.abs(w).max(1)
    if fmt == "e4m3":
        byte = np.frexp(amax)[1] - 1 + 127 - 7
    else:
        mant, ex = np.frexp(amax / 6.0)
        byte = np.where(mant > 0.5, ex, ex - 1) + 127
    byte = np.clip(np.where(amax > 0, byte, 1), 1, 254)
    scaled = (w * np.exp2(127.0 - byte)[:, None, :]).reshape(k, n).astype(np.float32)
    by_word = np.ascontiguousarray(scaled.reshape(k // 512, 128, 4, n).transpose(0, 1, 3, 2))
    if fmt == "e4m3":
        words = by_word.astype(ml_dtypes.float8_e4m3fn).view(np.uint8)
    else:
        c = by_word.astype(ml_dtypes.float4_e2m1fn).view(np.uint8) & 0xF
        words = (c[..., 0::2] | (c[..., 1::2] << 4)).reshape(k // 512, 128, 2 * n)
    return np.ascontiguousarray(words), np.ascontiguousarray(byte.astype(np.uint8).reshape(k // 512, 16, n))


def unpack_weight(words, scales, fmt):
    g, _, n = scales.shape
    words = np.ascontiguousarray(words).reshape(g, 128, n, -1)
    if fmt == "e4m3":
        vals = words.view(ml_dtypes.float8_e4m3fn).astype(np.float64)
    else:
        nib = np.empty((g, 128, n, 4), np.uint8)
        nib[..., 0::2] = words & 0xF
        nib[..., 1::2] = words >> 4
        vals = E2M1[nib]
    vals = vals * np.repeat(np.exp2(scales.astype(np.float64) - 127.0), 8, axis=1)[..., None]
    return vals.transpose(0, 1, 3, 2).reshape(g * 512, n)


def gelu(v):
    return 0.5 * v * (1.0 + np.tanh(np.sqrt(2.0 / np.pi) * (v + 0.044715 * v**3)))


K, K2, T, S, H, T2, P, N = 1024, 512, 2048, 512, 1024, 2048, 1024, 384

def setup_inputs():
    n = np.random.standard_normal
    s = mx_kscale(K)[:, None]
    s2 = mx_kscale(K2)[:, None]
    u = mx_kscale(H)[:, None]
    d = {}
    d["tab_words"], d["tab_scales"] = pack_weight(n((K, T)) * s, "e4m3")
    d["tab2_words"], d["tab2_scales"] = pack_weight(n((K2, T)) * s2, "e4m3")
    d["offs"] = striped(np.random.permutation(T)[:S])
    d["offs2"] = striped(np.random.permutation(T)[:S])
    perm = np.random.permutation(T2)
    d["offs3"] = striped(perm[:S])
    d["offs4"] = striped(perm[S:2 * S])
    d["offs5"] = striped(np.random.permutation(T2)[:P])
    d["w1"] = (n((K, H)) / s * u.T ** 2 * np.exp(0.8 * n((1, H))) / K ** 0.5).astype(np.float32)
    d["w2_words"], d["w2_scales"] = pack_weight(1.5 * n((K2, H)) / s2 / K2 ** 0.5, "e4m3")
    d["gain"] = (1.2 * np.exp(0.3 * n(H)) * u[:, 0]).astype(np.float32)
    d["page0"] = (0.9 * n((H, T2)) * u).astype(np.float32)
    d["wg1"] = np.exp(0.3 * n((128, S))).astype(np.float32)
    d["wg2"] = np.exp(0.3 * n((128, S))).astype(np.float32)
    d["shift"] = (0.5 * n(H) * u[:, 0]).astype(np.float32)
    d["w3"] = (0.46 * n((H, N)) / u / H ** 0.5).astype(np.float32)
    d["w4_words"], d["w4_scales"] = pack_weight(0.4 * n((H, N)) / u / H ** 0.5, "e2m1")
    return d

def reference(tab_words, tab_scales, tab2_words, tab2_scales, offs, offs2, offs3, offs4, offs5, w1, w2_words, w2_scales, gain, page0, wg1, wg2, shift, w3, w4_words, w4_scales):
    v = unpack_weight(tab_words, tab_scales, "e4m3")[:, unstriped(offs)]
    v2 = unpack_weight(tab2_words, tab2_scales, "e4m3")[:, unstriped(offs2)]
    h1 = np.sqrt(np.abs(mxq(f64(w1), 0, "e4m3").T @ v))
    h2 = f64(gain)[:, None] * np.tanh(unpack_weight(w2_words, w2_scales, "e4m3").T @ v2)
    page = f64(page0).copy()
    page[:, unstriped(offs3)] = np.tile(f64(wg1), (H // 128, 1)) * h1
    page[:, unstriped(offs4)] = np.tile(f64(wg2), (H // 128, 1)) * h2
    x = mxq(page[:, unstriped(offs5)] + f64(shift)[:, None], 0, "e4m3")
    wave = np.sin(mxq(f64(w3), 0, "e4m3").T @ x)
    line = unpack_weight(w4_words, w4_scales, "e2m1").T @ x
    return np.square(wave - line)

@@ -1,0 +1,302 @@
+import math
+from contextlib import ExitStack
+
+import concourse.mybir as mybir
+
+K, K2, T, S, H, T2, NJ, N = 1024, 512, 2048, 512, 1024, 2048, 1024, 384
+FLOPS = 2 * (K * H * S + K2 * H * S + 2 * H * N * NJ)
+
+F32 = mybir.dt.float32
+BF16 = mybir.dt.bfloat16
+I32 = mybir.dt.int32
+U32 = mybir.dt.uint32
+U16 = mybir.dt.uint16
+U8 = mybir.dt.uint8
+FP8X4 = mybir.dt.float8_e4m3fn_x4
+FP4X4 = mybir.dt.float4_e2m1fn_x4
+ALU = mybir.AluOpType
+ACT = mybir.ActivationFunctionType
+
+P = 128
+PACK = 4
+KP = P * PACK
+QUADS = (0, 2, 1, 3)
+TWO_PI = 2.0 * math.pi
+
+
+def tile_list_casing_slot_scores_kernel(
+    tc, tab_words, tab_scales, tab2_words, tab2_scales, offs, offs2, offs3, offs4, offs5,
+    w1, w2_words, w2_scales, gain, page0, wg1, wg2, shift, w3, w4_words, w4_scales, out,
+):
+    nc = tc.nc
+    with ExitStack() as ctx:
+        lists = ctx.enter_context(tc.tile_pool(name="lists", bufs=1))
+        sb = ctx.enter_context(tc.tile_pool(name="sb", bufs=1))
+        psum = ctx.enter_context(tc.psum_pool(name="psum", bufs=1))
+
+        def tile(shape, dtype, name, tag=None, bufs=1):
+            return sb.tile(shape, dtype, name=name, tag=tag or name, bufs=bufs, align_bytes=64)
+
+        def load_list(src, name):
+            t = lists.tile(list(src.shape), U16, name=name)
+            nc.sync.dma_start(t[:], src)
+            return t
+
+        def load_words(src, name, tag):
+            t = tile([P, src.shape[1]], U32, name, tag)
+            nc.sync.dma_start(out=t[:].bitcast(I32), in_=src.rearrange("p c i -> p (c i)").bitcast(I32))
+            return t
+
+        def zeroed(shape, name, eng):
+            t = tile(shape, U8, name)
+            eng.memset(t[:].bitcast(I32), 0)
+            return t
+
+        def load_page(i):
+            b, t = divmod(i, PACK)
+            pg = tile([P, T2], F32, "page%d" % i)
+            nc.sync.dma_start(out=pg[:], in_=page0[b * KP : (b + 1) * KP, :].rearrange("(p t) c -> p t c", t=PACK)[:, t, :])
+            return pg
+
+        def load_wg(src, t0, t1, name, tag=None):
+            t = tile([P, t1 - t0, S], F32, name, tag)
+            rows = src.rearrange("(p t) s -> p t s", t=PACK)[:, t0:t1, :]
+            for q in QUADS:
+                nc.sync.dma_start(out=t[32 * q : 32 * q + 32, :, :], in_=rows)
+            return t
+
+        def load_w1(a, b, tag):
+            t = tile([P, PACK, KP], F32, "w1_raw%d%d" % (a, b), tag)
+            nc.sync.dma_start(out=t[:], in_=w1[a * KP : (a + 1) * KP, b * KP : (b + 1) * KP].rearrange("(p j) c -> p j c", j=PACK))
+            return t
+
+        banks = [psum.tile([P, 512], F32, name="bank%d" % i) for i in range(8)]
+
+        tab2_sc = zeroed([P, T], "tab2_sc", nc.vector)
+        w2_sc = zeroed([P, H], "w2_sc", nc.vector)
+        tab_sc = zeroed([P, T], "tab_sc", nc.vector)
+        w4_sc = zeroed([P, 2 * N], "w4_sc", nc.vector)
+
+        def load_column(src, name):
+            t = tile([P, 2, PACK], F32, name)
+            nc.sync.dma_start(out=t[:], in_=src.rearrange("(b p t) -> p b t", b=2, t=PACK))
+            return t
+
+        idx2 = load_list(offs2, "idx2")
+        gain_sb = load_column(gain, "gain_sb")
+        tab2_w = load_words(tab2_words[0], "tab2_w", "sA")
+        for q in QUADS:
+            nc.scalar.dma_start(out=tab2_sc[32 * q : 32 * q + 4, :].bitcast(I32), in_=tab2_scales[0, 4 * q : 4 * q + 4, :].bitcast(I32))
+        w2_w = load_words(w2_words[0], "w2_w", "w2_w")
+        for q in QUADS:
+            nc.scalar.dma_start(out=w2_sc[32 * q : 32 * q + 4, :].bitcast(I32), in_=w2_scales[0, 4 * q : 4 * q + 4, :].bitcast(I32))
+        pages = {0: load_page(0)}
+        wg2_first = load_wg(wg2, 0, 1, "wg2_first")
+        idx4 = load_list(offs4, "idx4")
+        pages[4] = load_page(4)
+        wg2_rest = load_wg(wg2, 1, 4, "wg2_rest")
+        pages[1] = load_page(1)
+        pages[5] = load_page(5)
+        idx = load_list(offs, "idx")
+        tab_w = [load_words(tab_words[0], "tab_w0", "sB")]
+        pages[2] = load_page(2)
+        tab_w.append(load_words(tab_words[1], "tab_w1", "sC"))
+        for q in QUADS:
+            nc.sync.dma_start(out=tab_sc[32 * q : 32 * q + 8, :].bitcast(I32), in_=tab_scales[:, 4 * q : 4 * q + 4, :].bitcast(I32))
+        w1_raw = {(0, 0): load_w1(0, 0, "sD")}
+        pages[6] = load_page(6)
+        w1_raw[(1, 0)] = load_w1(1, 0, "sE")
+        pages[3] = load_page(3)
+        w1_raw[(0, 1)] = load_w1(0, 1, "sF")
+        pages[7] = load_page(7)
+        idx3 = load_list(offs3, "idx3")
+        wg1_first = load_wg(wg1, 0, 2, "wg1_first")
+
+        v2_w = tile([P, S], U32, "v2_w")
+        nc.vector.tensor_copy(out=v2_w[:], in_=tab2_w[:].indirect(idx2[:]))
+        v2_sc = tile([P, S], U8, "v2_sc")
+        nc.vector.tensor_copy(out=v2_sc[:], in_=tab2_sc[:].indirect(idx2[:]))
+
+        w2_wp = [tile([P, KP], U32, "w2_wp%d" % b) for b in range(2)]
+        w2_scp = [tile([P, KP], U8, "w2_scp%d" % b) for b in range(2)]
+        for b in range(2):
+            cols = slice(b * KP, (b + 1) * KP)
+            nc.vector.tensor_copy(
+                out=w2_wp[b][:].bitcast(I32).rearrange("p (t m) -> p m t", t=PACK),
+                in_=w2_w[:, cols].bitcast(I32).rearrange("p (m t) -> p m t", t=PACK),
+            )
+            nc.vector.tensor_copy(
+                out=w2_scp[b][:].rearrange("p (t m) -> p m t", t=PACK),
+                in_=w2_sc[:, cols].rearrange("p (m t) -> p m t", t=PACK),
+            )
+
+        def wg2_of(t):
+            return wg2_first[:, 0, :] if t == 0 else wg2_rest[:, t - 1, :]
+
+        hs = [tile([P, S], F32, "h%d" % i) for i in range(8)]
+        for i in (0, 4, 1, 5, 2, 6, 3, 7):
+            b, t = divmod(i, PACK)
+            cols = slice(t * P, (t + 1) * P)
+            nc.tensor.matmul_mx(
+                out=banks[7][:], lhsT=w2_wp[b][:, cols].bitcast(FP8X4), lhsT_scale=w2_scp[b][:, cols],
+                rhs=v2_w[:].bitcast(FP8X4), rhs_scale=v2_sc[:], start=True, stop=True,
+            )
+            nc.scalar.activation(out=hs[i][:], in_=banks[7][:], func=ACT.Tanh)
+            nc.scalar.activation(out=hs[i][:], in_=hs[i][:], func=ACT.Copy, scale=gain_sb[:, b, t : t + 1])
+            nc.vector.tensor_tensor(out=pages[i][:].indirect(idx4[:]), in0=hs[i][:], in1=wg2_of(t), op=ALU.mult)
+
+        v_w = []
+        for a in range(2):
+            vw = tile([P, S], U32, "v_w%d" % a)
+            nc.vector.tensor_copy(out=vw[:], in_=tab_w[a][:].indirect(idx[:]))
+            v_w.append(vw)
+        v_sc = tile([P, S], U8, "v_sc")
+        nc.vector.tensor_copy(out=v_sc[:], in_=tab_sc[:].indirect(idx[:]))
+
+        def load_w3(a, tag):
+            raw = tile([P, PACK, N], F32, "w3_raw%d" % a, tag)
+            nc.sync.dma_start(out=raw[:], in_=w3[a * KP : (a + 1) * KP, :].rearrange("(p j) n -> p j n", j=PACK))
+            return raw
+
+        w1_raw[(1, 1)] = load_w1(1, 1, "sA")
+        idx5 = load_list(offs5, "idx5")
+        shift_sb = load_column(shift, "shift_sb")
+        w3_raw = [load_w3(0, "sB")]
+        wg1_rest = load_wg(wg1, 2, 4, "wg1_rest")
+        w3_raw.append(load_w3(1, "sC"))
+        w4_w = tile([P, 2, 2 * N], U8, "w4_w")
+        nc.sync.dma_start(out=w4_w[:].bitcast(I32), in_=w4_words.rearrange("a p c -> p a c").bitcast(I32))
+        for q in QUADS:
+            nc.sync.dma_start(
+                out=w4_sc[32 * q : 32 * q + 4, :].bitcast(I32).rearrange("p (a n) -> p a n", a=2),
+                in_=w4_scales[:, 4 * q : 4 * q + 4, :].rearrange("a r n -> r a n").bitcast(I32),
+            )
+
+        w1_q, w1_s, h1 = {}, {}, {}
+
+        def quantize_w1(a, b):
+            grouped = tile([P, KP * PACK], BF16, "w1_bf%d%d" % (a, b), "wbf", 2)
+            nc.scalar.copy(
+                out=grouped[:].rearrange("p (t m j) -> p m j t", t=PACK, j=PACK),
+                in_=w1_raw[(a, b)][:].rearrange("p j (m t) -> p m j t", t=PACK),
+            )
+            w1_q[(a, b)] = tile([P, KP], U32, "w1_q%d%d" % (a, b))
+            w1_s[(a, b)] = tile([P, KP], U8, "w1_s%d%d" % (a, b))
+            nc.vector.quantize_mx(out=w1_q[(a, b)][:].bitcast(FP8X4), scales=w1_s[(a, b)][:], in_=grouped[:])
+
+        def make_h1(i):
+            b, t = divmod(i, PACK)
+            cols = slice(t * P, (t + 1) * P)
+            for a in range(2):
+                nc.tensor.matmul_mx(
+                    out=banks[i][:], lhsT=w1_q[(a, b)][:, cols].bitcast(FP8X4), lhsT_scale=w1_s[(a, b)][:, cols],
+                    rhs=v_w[a][:].bitcast(FP8X4), rhs_scale=v_sc[4 * a : P, :], start=(a == 0), stop=(a == 1),
+                )
+            h1[i] = tile([P, S], F32, "h1_%d" % i, "h%d" % (4 * (i % 2)))
+            nc.scalar.activation(out=h1[i][:], in_=banks[i][:], func=ACT.Abs)
+            nc.scalar.activation(out=h1[i][:], in_=h1[i][:], func=ACT.Sqrt)
+
+        w3_bf = tile([P, 2 * N * PACK], BF16, "w3_bf")
+        w3_q = tile([P, 2 * N], U32, "w3_q")
+        w3_s = tile([P, 2 * N], U8, "w3_s")
+
+        def round_w3(a):
+            nc.scalar.copy(
+                out=w3_bf[:, a * N * PACK : (a + 1) * N * PACK].rearrange("p (c i j) -> p c j i", i=4, j=PACK),
+                in_=w3_raw[a][:].rearrange("p j (c i) -> p c j i", i=4),
+            )
+
+        def quantize_w3():
+            for c0, c1 in ((0, 512), (512, 2 * N)):
+                nc.vector.quantize_mx(out=w3_q[:, c0:c1].bitcast(FP8X4), scales=w3_s[:, c0:c1], in_=w3_bf[:, PACK * c0 : PACK * c1])
+
+        x_q = {(b, h): tile([P, 512], U32, "x_q%d%d" % (b, h)) for b in range(2) for h in range(2)}
+        x_s = {(b, h): tile([P, 512], U8, "x_s%d%d" % (b, h)) for b in range(2) for h in range(2)}
+        units = [(h, n) for h in range(2) for n in range(3)]
+        unit_banks = [(0, 1), (2, 3), (4, 5), (6, 7), (0, 1), (2, 3)]
+
+        def unit_pass(u, b):
+            h, n = units[u]
+            bank_a, bank_l = unit_banks[u]
+            c0 = b * N + n * P
+            nc.tensor.matmul_mx(
+                out=banks[bank_a][:], lhsT=w3_q[:, c0 : c0 + P].bitcast(FP8X4), lhsT_scale=w3_s[:, c0 : c0 + P],
+                rhs=x_q[(b, h)][:].bitcast(FP8X4), rhs_scale=x_s[(b, h)][:], start=(b == 0), stop=(b == 1),
+            )
+            nc.tensor.matmul_mx(
+                out=banks[bank_l][:], lhsT=w4_w[:, b, 2 * n * P : 2 * (n + 1) * P].bitcast(FP4X4), lhsT_scale=w4_sc[:, c0 : c0 + P],
+                rhs=x_q[(b, h)][:].bitcast(FP8X4), rhs_scale=x_s[(b, h)][:], start=(b == 0), stop=(b == 1),
+            )
+
+        def quantize_x(b, h, grouped):
+            nc.vector.quantize_mx(out=x_q[(b, h)][:].bitcast(FP8X4), scales=x_s[(b, h)][:], in_=grouped.rearrange("p c t -> p (c t)"))
+
+        picked = {}
+
+        def put_and_pick(i, piece):
+            nc.vector.tensor_tensor(out=pages[i][:].indirect(idx3[:]), in0=h1[i][:], in1=(wg1_first if i % PACK < 2 else wg1_rest)[:, i % 2, :], op=ALU.mult)
+            picked[i] = tile([P, NJ], F32, "picked%d" % i, "picked", 2)
+            for c0 in range(0, NJ, piece):
+                nc.vector.tensor_copy(out=picked[i][:, c0 : c0 + piece], in_=pages[i][:].indirect(idx5[:, c0 // 16 : (c0 + piece) // 16]))
+
+        x_planes = tile([P, PACK, NJ], BF16, "x_planes", "sD")
+        x0 = tile([P, NJ, PACK], BF16, "x0", "sE")
+        x1 = [tile([P, 512, PACK], BF16, "x1_%d" % h) for h in range(2)]
+
+        def shift_plane(t):
+            nc.scalar.activation(out=x_planes[:, t, :], in_=picked[t][:], func=ACT.Identity, bias=shift_sb[:, 0, t : t + 1])
+
+        def weave_x0(h):
+            cols = slice(h * 512, (h + 1) * 512)
+            nc.scalar.copy(
+                out=x0[:, cols, :].rearrange("p (c i) t -> p c t i", i=4),
+                in_=x_planes[:, :, cols].rearrange("p t (c i) -> p c t i", i=4),
+            )
+            quantize_x(0, h, x0[:, cols, :])
+
+        def shift_into_x1(t, piece):
+            for c0 in range(0, NJ, piece):
+                h, c = divmod(c0, 512)
+                nc.scalar.activation(out=x1[h][:, c : c + piece, t], in_=picked[PACK + t][:, c0 : c0 + piece], func=ACT.Identity, bias=shift_sb[:, 1, t : t + 1])
+
+        quantize_w1(0, 0)
+        quantize_w1(1, 0)
+        quantize_w1(0, 1)
+        quantize_w1(1, 1)
+        make_h1(0)
+        make_h1(1)
+        for i in range(8):
+            put_and_pick(i, 256 if i == 7 else NJ)
+            if i + 2 < 8:
+                make_h1(i + 2)
+            if i == 1:
+                round_w3(0)
+            if i == 2:
+                round_w3(1)
+                quantize_w3()
+            if i < 4:
+                shift_plane(i)
+            else:
+                shift_into_x1(i - 4, 256 if i == 7 else 512)
+            if i in (3, 4):
+                weave_x0(i - 3)
+            if i == 5:
+                for u in range(4):
+                    unit_pass(u, 0)
+
+        angles = [tile([P, 3, 512], F32, "angle%d" % h, tag) for h, tag in ((0, "wg2_rest"), (1, "w3_bf"))]
+        diffs = [tile([P, 3, 512], F32, "diff%d" % h, tag) for h, tag in ((0, "sA"), (1, "sB"))]
+        for u, (h, n) in enumerate(units):
+            if n == 0:
+                quantize_x(1, h, x1[h][:])
+            if u >= 4:
+                unit_pass(u, 0)
+            unit_pass(u, 1)
+            bank_a, bank_l = unit_banks[u]
+            turns = tile([P, 512], I32, "turns%d" % u, "h%d" % (1, 2, 3, 5, 6, 7)[u])
+            nc.vector.tensor_scalar(out=turns[:], in0=banks[bank_a][:], scalar1=1.0 / TWO_PI, scalar2=0.5, op0=ALU.mult, op1=ALU.add)
+            nc.vector.scalar_tensor_tensor(out=angles[h][:, n, :], in0=turns[:], scalar=-TWO_PI, in1=banks[bank_a][:], op0=ALU.mult, op1=ALU.add)
+            nc.scalar.activation(out=angles[h][:, n, :], in_=angles[h][:, n, :], func=ACT.Sin, scale=-1.0, bias=-math.pi)
+            nc.vector.tensor_tensor(out=diffs[h][:, n, :], in0=banks[bank_l][:], in1=angles[h][:, n, :], op=ALU.subtract)
+            nc.scalar.activation(out=diffs[h][:, n, :], in_=diffs[h][:, n, :], func=ACT.Square)
+            nc.sync.dma_start(out=out[n * P : (n + 1) * P, h * 512 : (h + 1) * 512], in_=diffs[h][:, n, :])

@@ -2,6 +2,7 @@ import math
 from contextlib import ExitStack
 
 import concourse.mybir as mybir
+from concourse.masks import make_identity
 
 K, K2, T, S, H, T2, NJ, N = 1024, 512, 2048, 512, 1024, 2048, 1024, 384
 FLOPS = 2 * (K * H * S + K2 * H * S + 2 * H * N * NJ)
@@ -20,8 +21,11 @@ ACT = mybir.ActivationFunctionType
 P = 128
 PACK = 4
 KP = P * PACK
-QUADS = (0, 2, 1, 3)
+QUAD = 32
 TWO_PI = 2.0 * math.pi
+WHOLE = 1.5 * 2.0**23
+SCALAR_TURNS = (2,4,)
+GPSIMD_SQUARES = ()
 
 
 def tile_list_casing_slot_scores_kernel(
@@ -47,10 +51,15 @@ def tile_list_casing_slot_scores_kernel(
             nc.sync.dma_start(out=t[:].bitcast(I32), in_=src.rearrange("p c i -> p (c i)").bitcast(I32))
             return t
 
-        def zeroed(shape, name, eng):
-            t = tile(shape, U8, name)
+        def zeroed(width, name, eng):
+            t = tile([P, width], U8, name)
             eng.memset(t[:].bitcast(I32), 0)
             return t
+
+        def load_scale_rows(plane, src, a=0, quads=range(4)):
+            for q in quads:
+                first = QUAD * q + 4 * a
+                nc.sync.dma_start(out=plane[first : first + 4, :].bitcast(I32), in_=src[a, 4 * q : 4 * q + 4, :].bitcast(I32))
 
         def load_page(i):
             b, t = divmod(i, PACK)
@@ -58,59 +67,59 @@ def tile_list_casing_slot_scores_kernel(
             nc.sync.dma_start(out=pg[:], in_=page0[b * KP : (b + 1) * KP, :].rearrange("(p t) c -> p t c", t=PACK)[:, t, :])
             return pg
 
-        def load_wg(src, t0, t1, name, tag=None):
-            t = tile([P, t1 - t0, S], F32, name, tag)
-            rows = src.rearrange("(p t) s -> p t s", t=PACK)[:, t0:t1, :]
-            for q in QUADS:
-                nc.sync.dma_start(out=t[32 * q : 32 * q + 32, :, :], in_=rows)
+        def load_plain(src, name, tag):
+            t = tile(list(src.shape), F32, name, tag)
+            nc.sync.dma_start(out=t[:], in_=src)
             return t
 
         def load_w1(a, b, tag):
-            t = tile([P, PACK, KP], F32, "w1_raw%d%d" % (a, b), tag)
-            nc.sync.dma_start(out=t[:], in_=w1[a * KP : (a + 1) * KP, b * KP : (b + 1) * KP].rearrange("(p j) c -> p j c", j=PACK))
-            return t
+            return load_plain(w1[a * KP : (a + 1) * KP, b * KP : (b + 1) * KP].rearrange("(p j) c -> p j c", j=PACK), "w1_raw%d%d" % (a, b), tag)
+
+        def load_w3(a, tag):
+            return load_plain(w3[a * KP : (a + 1) * KP, :].rearrange("(p j) n -> p j n", j=PACK), "w3_raw%d" % a, tag)
+
+        def load_column(src, name):
+            return load_plain(src.rearrange("(b p t) -> p b t", b=2, t=PACK), name, name)
 
         banks = [psum.tile([P, 512], F32, name="bank%d" % i) for i in range(8)]
 
-        tab2_sc = zeroed([P, T], "tab2_sc", nc.vector)
-        w2_sc = zeroed([P, H], "w2_sc", nc.vector)
-        tab_sc = zeroed([P, T], "tab_sc", nc.vector)
-        w4_sc = zeroed([P, 2 * N], "w4_sc", nc.vector)
+        tab2_sc = zeroed(T, "tab2_sc", nc.vector)
+        w2_sc = zeroed(H, "w2_sc", nc.vector)
+        ident = tile([P, P], F32, "ident")
+        make_identity(nc, ident[:])
+        tab_sc = zeroed(T, "tab_sc", nc.gpsimd)
+        w4_sc = zeroed(2 * N, "w4_sc", nc.gpsimd)
 
-        def load_column(src, name):
-            t = tile([P, 2, PACK], F32, name)
-            nc.sync.dma_start(out=t[:], in_=src.rearrange("(b p t) -> p b t", b=2, t=PACK))
-            return t
-
+        pages, w2_w, tab_w, w1_raw = {}, {}, {}, {}
         idx2 = load_list(offs2, "idx2")
         gain_sb = load_column(gain, "gain_sb")
+        wg2_rows = load_plain(wg2, "wg2_rows", "x_q00")
+        load_scale_rows(tab2_sc, tab2_scales)
         tab2_w = load_words(tab2_words[0], "tab2_w", "sA")
-        for q in QUADS:
-            nc.scalar.dma_start(out=tab2_sc[32 * q : 32 * q + 4, :].bitcast(I32), in_=tab2_scales[0, 4 * q : 4 * q + 4, :].bitcast(I32))
-        w2_w = load_words(w2_words[0], "w2_w", "w2_w")
-        for q in QUADS:
-            nc.scalar.dma_start(out=w2_sc[32 * q : 32 * q + 4, :].bitcast(I32), in_=w2_scales[0, 4 * q : 4 * q + 4, :].bitcast(I32))
-        pages = {0: load_page(0)}
-        wg2_first = load_wg(wg2, 0, 1, "wg2_first")
+        w2_w[0] = load_words(w2_words[0, :, 0:KP, :], "w2_w0", "w2_w0")
+        load_scale_rows(w2_sc, w2_scales)
+        pages[0] = load_page(0)
         idx4 = load_list(offs4, "idx4")
-        pages[4] = load_page(4)
-        wg2_rest = load_wg(wg2, 1, 4, "wg2_rest")
+        w2_w[1] = load_words(w2_words[0, :, KP:H, :], "w2_w1", "w2_w1")
         pages[1] = load_page(1)
-        pages[5] = load_page(5)
-        idx = load_list(offs, "idx")
-        tab_w = [load_words(tab_words[0], "tab_w0", "sB")]
         pages[2] = load_page(2)
-        tab_w.append(load_words(tab_words[1], "tab_w1", "sC"))
-        for q in QUADS:
-            nc.sync.dma_start(out=tab_sc[32 * q : 32 * q + 8, :].bitcast(I32), in_=tab_scales[:, 4 * q : 4 * q + 4, :].bitcast(I32))
-        w1_raw = {(0, 0): load_w1(0, 0, "sD")}
+        load_scale_rows(tab_sc, tab_scales, 0, range(0, 2))
+        wg1_rows = load_plain(wg1, "wg1_rows", "x_q01")
+        pages[3] = load_page(3)
+        load_scale_rows(tab_sc, tab_scales, 0, range(2, 4))
+        idx = load_list(offs, "idx")
+        tab_w[0] = load_words(tab_words[0], "tab_w0", "sB")
+        load_scale_rows(tab_sc, tab_scales, 1, range(0, 2))
+        pages[4] = load_page(4)
+        load_scale_rows(tab_sc, tab_scales, 1, range(2, 4))
+        tab_w[1] = load_words(tab_words[1], "tab_w1", "sC")
+        pages[5] = load_page(5)
+        w1_raw[(0, 0)] = load_w1(0, 0, "sD")
         pages[6] = load_page(6)
         w1_raw[(1, 0)] = load_w1(1, 0, "sE")
-        pages[3] = load_page(3)
-        w1_raw[(0, 1)] = load_w1(0, 1, "sF")
         pages[7] = load_page(7)
         idx3 = load_list(offs3, "idx3")
-        wg1_first = load_wg(wg1, 0, 2, "wg1_first")
+        w1_raw[(0, 1)] = load_w1(0, 1, "sF")
 
         v2_w = tile([P, S], U32, "v2_w")
         nc.vector.tensor_copy(out=v2_w[:], in_=tab2_w[:].indirect(idx2[:]))
@@ -123,27 +132,49 @@ def tile_list_casing_slot_scores_kernel(
             cols = slice(b * KP, (b + 1) * KP)
             nc.vector.tensor_copy(
                 out=w2_wp[b][:].bitcast(I32).rearrange("p (t m) -> p m t", t=PACK),
-                in_=w2_w[:, cols].bitcast(I32).rearrange("p (m t) -> p m t", t=PACK),
+                in_=w2_w[b][:].bitcast(I32).rearrange("p (m t) -> p m t", t=PACK),
             )
             nc.vector.tensor_copy(
                 out=w2_scp[b][:].rearrange("p (t m) -> p m t", t=PACK),
                 in_=w2_sc[:, cols].rearrange("p (m t) -> p m t", t=PACK),
             )
 
-        def wg2_of(t):
-            return wg2_first[:, 0, :] if t == 0 else wg2_rest[:, t - 1, :]
+        def turn(rows, bank):
+            for c in range(4):
+                nc.tensor.transpose(bank[:, c * P : (c + 1) * P], rows[:, c * P : (c + 1) * P], ident[:])
 
-        hs = [tile([P, S], F32, "h%d" % i) for i in range(8)]
-        for i in (0, 4, 1, 5, 2, 6, 3, 7):
+        def deal(turned, t, bank, name, tag):
+            spread = tile([P, S], F32, name, tag)
+            nc.scalar.copy(
+                out=spread[:].rearrange("j (c q p) -> j c q p", c=4, q=4),
+                in_=turned[:].rearrange("j (c p t) -> j c p t", c=4, t=PACK)[:, :, :, t].unsqueeze(2).to_broadcast([P, 4, 4, QUAD]),
+            )
+            turn(spread, bank)
+
+        turn(wg2_rows, banks[0])
+        wg2g, h2 = {}, {}
+        for i in range(8):
             b, t = divmod(i, PACK)
+            if b == 0:
+                deal(banks[0], t, banks[1 + t], "wg2_spread%d" % t, "x_q10" if t == 0 else "w2_sc")
             cols = slice(t * P, (t + 1) * P)
             nc.tensor.matmul_mx(
-                out=banks[7][:], lhsT=w2_wp[b][:, cols].bitcast(FP8X4), lhsT_scale=w2_scp[b][:, cols],
+                out=banks[6 + i % 2][:], lhsT=w2_wp[b][:, cols].bitcast(FP8X4), lhsT_scale=w2_scp[b][:, cols],
                 rhs=v2_w[:].bitcast(FP8X4), rhs_scale=v2_sc[:], start=True, stop=True,
             )
-            nc.scalar.activation(out=hs[i][:], in_=banks[7][:], func=ACT.Tanh)
-            nc.scalar.activation(out=hs[i][:], in_=hs[i][:], func=ACT.Copy, scale=gain_sb[:, b, t : t + 1])
-            nc.vector.tensor_tensor(out=pages[i][:].indirect(idx4[:]), in0=hs[i][:], in1=wg2_of(t), op=ALU.mult)
+            wg2g[i] = tile([P, S], F32, "wg2g%d" % i)
+            nc.scalar.activation(out=wg2g[i][:], in_=banks[1 + t][:], func=ACT.Copy, scale=gain_sb[:, b, t : t + 1])
+            h2[i] = tile([P, S], F32, "h%d" % i)
+            nc.scalar.activation(out=h2[i][:], in_=banks[6 + i % 2][:], func=ACT.Tanh)
+            nc.vector.tensor_tensor(out=pages[i][:].indirect(idx4[:]), in0=h2[i][:], in1=wg2g[i][:], op=ALU.mult)
+
+        turn(wg1_rows, banks[5])
+        wg1_sb = []
+        for t in range(PACK):
+            deal(banks[5], t, banks[t], "wg1_spread%d" % t, "x_q1%d" % (t % 2))
+            dealt = tile([P, S], F32, "wg1_%d" % t)
+            nc.scalar.copy(out=dealt[:], in_=banks[t][:])
+            wg1_sb.append(dealt)
 
         v_w = []
         for a in range(2):
@@ -153,22 +184,15 @@ def tile_list_casing_slot_scores_kernel(
         v_sc = tile([P, S], U8, "v_sc")
         nc.vector.tensor_copy(out=v_sc[:], in_=tab_sc[:].indirect(idx[:]))
 
-        def load_w3(a, tag):
-            raw = tile([P, PACK, N], F32, "w3_raw%d" % a, tag)
-            nc.sync.dma_start(out=raw[:], in_=w3[a * KP : (a + 1) * KP, :].rearrange("(p j) n -> p j n", j=PACK))
-            return raw
-
         w1_raw[(1, 1)] = load_w1(1, 1, "sA")
         idx5 = load_list(offs5, "idx5")
         shift_sb = load_column(shift, "shift_sb")
-        w3_raw = [load_w3(0, "sB")]
-        wg1_rest = load_wg(wg1, 2, 4, "wg1_rest")
-        w3_raw.append(load_w3(1, "sC"))
+        w3_raw = [load_w3(0, "sB"), load_w3(1, "sC")]
         w4_w = tile([P, 2, 2 * N], U8, "w4_w")
         nc.sync.dma_start(out=w4_w[:].bitcast(I32), in_=w4_words.rearrange("a p c -> p a c").bitcast(I32))
-        for q in QUADS:
+        for q in range(4):
             nc.sync.dma_start(
-                out=w4_sc[32 * q : 32 * q + 4, :].bitcast(I32).rearrange("p (a n) -> p a n", a=2),
+                out=w4_sc[QUAD * q : QUAD * q + 4, :].bitcast(I32).rearrange("p (a n) -> p a n", a=2),
                 in_=w4_scales[:, 4 * q : 4 * q + 4, :].rearrange("a r n -> r a n").bitcast(I32),
             )
 
@@ -192,7 +216,7 @@ def tile_list_casing_slot_scores_kernel(
                     out=banks[i][:], lhsT=w1_q[(a, b)][:, cols].bitcast(FP8X4), lhsT_scale=w1_s[(a, b)][:, cols],
                     rhs=v_w[a][:].bitcast(FP8X4), rhs_scale=v_sc[4 * a : P, :], start=(a == 0), stop=(a == 1),
                 )
-            h1[i] = tile([P, S], F32, "h1_%d" % i, "h%d" % (4 * (i % 2)))
+            h1[i] = tile([P, S], F32, "h1_%d" % i, "h%d" % (i % 2))
             nc.scalar.activation(out=h1[i][:], in_=banks[i][:], func=ACT.Abs)
             nc.scalar.activation(out=h1[i][:], in_=h1[i][:], func=ACT.Sqrt)
 
@@ -210,41 +234,47 @@ def tile_list_casing_slot_scores_kernel(
             for c0, c1 in ((0, 512), (512, 2 * N)):
                 nc.vector.quantize_mx(out=w3_q[:, c0:c1].bitcast(FP8X4), scales=w3_s[:, c0:c1], in_=w3_bf[:, PACK * c0 : PACK * c1])
 
-        x_q = {(b, h): tile([P, 512], U32, "x_q%d%d" % (b, h)) for b in range(2) for h in range(2)}
-        x_s = {(b, h): tile([P, 512], U8, "x_s%d%d" % (b, h)) for b in range(2) for h in range(2)}
+        x_q, x_s = {}, {}
         units = [(h, n) for h in range(2) for n in range(3)]
-        unit_banks = [(0, 1), (2, 3), (4, 5), (6, 7), (0, 1), (2, 3)]
+        unit_banks = [(0, 1), (2, 3), (4, 5), (6, 7), (0, 2), (4, 6)]
 
-        def unit_pass(u, b):
+        def wave_pass(u, b):
             h, n = units[u]
-            bank_a, bank_l = unit_banks[u]
             c0 = b * N + n * P
             nc.tensor.matmul_mx(
-                out=banks[bank_a][:], lhsT=w3_q[:, c0 : c0 + P].bitcast(FP8X4), lhsT_scale=w3_s[:, c0 : c0 + P],
+                out=banks[unit_banks[u][0]][:], lhsT=w3_q[:, c0 : c0 + P].bitcast(FP8X4), lhsT_scale=w3_s[:, c0 : c0 + P],
                 rhs=x_q[(b, h)][:].bitcast(FP8X4), rhs_scale=x_s[(b, h)][:], start=(b == 0), stop=(b == 1),
             )
+
+        def line_pass(u, b):
+            h, n = units[u]
+            c0 = b * N + n * P
             nc.tensor.matmul_mx(
-                out=banks[bank_l][:], lhsT=w4_w[:, b, 2 * n * P : 2 * (n + 1) * P].bitcast(FP4X4), lhsT_scale=w4_sc[:, c0 : c0 + P],
+                out=banks[unit_banks[u][1]][:], lhsT=w4_w[:, b, 2 * n * P : 2 * (n + 1) * P].bitcast(FP4X4), lhsT_scale=w4_sc[:, c0 : c0 + P],
                 rhs=x_q[(b, h)][:].bitcast(FP8X4), rhs_scale=x_s[(b, h)][:], start=(b == 0), stop=(b == 1),
             )
 
         def quantize_x(b, h, grouped):
+            x_q[(b, h)] = tile([P, 512], U32, "x_q%d%d" % (b, h))
+            x_s[(b, h)] = tile([P, 512], U8, "x_s%d%d" % (b, h))
             nc.vector.quantize_mx(out=x_q[(b, h)][:].bitcast(FP8X4), scales=x_s[(b, h)][:], in_=grouped.rearrange("p c t -> p (c t)"))
 
         picked = {}
 
-        def put_and_pick(i, piece):
-            nc.vector.tensor_tensor(out=pages[i][:].indirect(idx3[:]), in0=h1[i][:], in1=(wg1_first if i % PACK < 2 else wg1_rest)[:, i % 2, :], op=ALU.mult)
-            picked[i] = tile([P, NJ], F32, "picked%d" % i, "picked", 2)
-            for c0 in range(0, NJ, piece):
-                nc.vector.tensor_copy(out=picked[i][:, c0 : c0 + piece], in_=pages[i][:].indirect(idx5[:, c0 // 16 : (c0 + piece) // 16]))
+        def put(i):
+            nc.vector.tensor_tensor(out=pages[i][:].indirect(idx3[:]), in0=h1[i][:], in1=wg1_sb[i % PACK][:], op=ALU.mult)
+
+        def pick(i, c0, c1, piece, tag="picked", bufs=2):
+            picked[(i, c0)] = tile([P, c1 - c0], F32, "picked%d_%d" % (i, c0), tag, bufs)
+            for c in range(c0, c1, piece):
+                nc.vector.tensor_copy(out=picked[(i, c0)][:, c - c0 : c - c0 + piece], in_=pages[i][:].indirect(idx5[:, c // 16 : (c + piece) // 16]))
 
         x_planes = tile([P, PACK, NJ], BF16, "x_planes", "sD")
         x0 = tile([P, NJ, PACK], BF16, "x0", "sE")
         x1 = [tile([P, 512, PACK], BF16, "x1_%d" % h) for h in range(2)]
 
         def shift_plane(t):
-            nc.scalar.activation(out=x_planes[:, t, :], in_=picked[t][:], func=ACT.Identity, bias=shift_sb[:, 0, t : t + 1])
+            nc.scalar.activation(out=x_planes[:, t, :], in_=picked[(t, 0)][:], func=ACT.Identity, bias=shift_sb[:, 0, t : t + 1])
 
         def weave_x0(h):
             cols = slice(h * 512, (h + 1) * 512)
@@ -254,11 +284,16 @@ def tile_list_casing_slot_scores_kernel(
             )
             quantize_x(0, h, x0[:, cols, :])
 
-        def shift_into_x1(t, piece):
-            for c0 in range(0, NJ, piece):
-                h, c = divmod(c0, 512)
-                nc.scalar.activation(out=x1[h][:, c : c + piece, t], in_=picked[PACK + t][:, c0 : c0 + piece], func=ACT.Identity, bias=shift_sb[:, 1, t : t + 1])
+        def shift_into_x1(t, c0, c1, piece):
+            for c in range(c0, c1, piece):
+                h, col = divmod(c, 512)
+                nc.scalar.activation(
+                    out=x1[h][:, col : col + piece, t], in_=picked[(PACK + t, c0)][:, c - c0 : c - c0 + piece],
+                    func=ACT.Identity, bias=shift_sb[:, 1, t : t + 1],
+                )
 
+        warm_sqrt = tile([P, 1], F32, "warm_sqrt")
+        nc.scalar.activation(out=warm_sqrt[:], in_=h2[7][:, 0:1], func=ACT.Sqrt, scale=0.0, bias=1.0)
         quantize_w1(0, 0)
         quantize_w1(1, 0)
         quantize_w1(0, 1)
@@ -266,9 +301,18 @@ def tile_list_casing_slot_scores_kernel(
         make_h1(0)
         make_h1(1)
         for i in range(8):
-            put_and_pick(i, 256 if i == 7 else NJ)
+            width = 512 if i == 6 else NJ
+            put(i)
+            if i < 7:
+                pick(i, 0, width, width)
+            else:
+                pick(i, 0, 512, 256)
+                pick(i, 512, NJ, 256)
             if i + 2 < 8:
                 make_h1(i + 2)
+            if i == 5:
+                warm_sin = tile([P, 1], F32, "warm_sin")
+                nc.scalar.activation(out=warm_sin[:], in_=h1[7][:, 0:1], func=ACT.Sin, scale=0.0)
             if i == 1:
                 round_w3(0)
             if i == 2:
@@ -277,26 +321,70 @@ def tile_list_casing_slot_scores_kernel(
             if i < 4:
                 shift_plane(i)
             else:
-                shift_into_x1(i - 4, 256 if i == 7 else 512)
+                if i < 7:
+                    shift_into_x1(i - 4, 0, width, 512)
+                else:
+                    shift_into_x1(3, 0, 512, 256)
+                    shift_into_x1(3, 512, NJ, 256)
             if i in (3, 4):
                 weave_x0(i - 3)
             if i == 5:
                 for u in range(4):
-                    unit_pass(u, 0)
+                    wave_pass(u, 0)
+                    line_pass(u, 0)
 
-        angles = [tile([P, 3, 512], F32, "angle%d" % h, tag) for h, tag in ((0, "wg2_rest"), (1, "w3_bf"))]
-        diffs = [tile([P, 3, 512], F32, "diff%d" % h, tag) for h, tag in ((0, "sA"), (1, "sB"))]
-        for u, (h, n) in enumerate(units):
-            if n == 0:
-                quantize_x(1, h, x1[h][:])
-            if u >= 4:
-                unit_pass(u, 0)
-            unit_pass(u, 1)
-            bank_a, bank_l = unit_banks[u]
-            turns = tile([P, 512], I32, "turns%d" % u, "h%d" % (1, 2, 3, 5, 6, 7)[u])
-            nc.vector.tensor_scalar(out=turns[:], in0=banks[bank_a][:], scalar1=1.0 / TWO_PI, scalar2=0.5, op0=ALU.mult, op1=ALU.add)
-            nc.vector.scalar_tensor_tensor(out=angles[h][:, n, :], in0=turns[:], scalar=-TWO_PI, in1=banks[bank_a][:], op0=ALU.mult, op1=ALU.add)
-            nc.scalar.activation(out=angles[h][:, n, :], in_=angles[h][:, n, :], func=ACT.Sin, scale=-1.0, bias=-math.pi)
-            nc.vector.tensor_tensor(out=diffs[h][:, n, :], in0=banks[bank_l][:], in1=angles[h][:, n, :], op=ALU.subtract)
-            nc.scalar.activation(out=diffs[h][:, n, :], in_=diffs[h][:, n, :], func=ACT.Square)
-            nc.sync.dma_start(out=out[n * P : (n + 1) * P, h * 512 : (h + 1) * 512], in_=diffs[h][:, n, :])
+        angles, diffs = {}, {}
+
+        def reduce_angle(u):
+            bank_a = banks[unit_banks[u][0]]
+            tag = "h%d" % (u + 2)
+            if u in SCALAR_TURNS:
+                biased = tile([P, 512], U32, "biased%d" % u, "wg1_%d" % (u % 4))
+                nc.scalar.activation(out=biased[:], in_=bank_a[:], func=ACT.Copy, scale=1.0 / TWO_PI, bias=WHOLE)
+                turns = tile([P, 512], F32, "turns%d" % u, tag)
+                nc.scalar.activation(out=turns[:], in_=biased[:], func=ACT.Copy, bias=-WHOLE)
+            else:
+                turns = tile([P, 512], I32, "turns%d" % u, tag)
+                nc.vector.tensor_scalar(out=turns[:], in0=bank_a[:], scalar1=1.0 / TWO_PI, scalar2=None, op0=ALU.mult)
+            angles[u] = tile([P, 512], F32, "angle%d" % u, "wg2g%d" % u)
+            nc.vector.scalar_tensor_tensor(out=angles[u][:], in0=turns[:], scalar=-TWO_PI, in1=bank_a[:], op0=ALU.mult, op1=ALU.add)
+            nc.scalar.activation(out=angles[u][:], in_=angles[u][:], func=ACT.Sin)
+
+        def score(u, piece):
+            h, n = units[u]
+            diffs[u] = tile([P, 512], F32, "diff%d" % u, ("sA", "sB", "sC", "sF", "w3_bf", "v_w0")[u])
+            for c in range(0, 512, piece):
+                part = diffs[u][:, c : c + piece]
+                nc.vector.tensor_tensor(out=part, in0=banks[unit_banks[u][1]][:, c : c + piece], in1=angles[u][:, c : c + piece], op=ALU.subtract)
+                if u in GPSIMD_SQUARES:
+                    nc.gpsimd.tensor_tensor(out=part, in0=part, in1=part, op=ALU.mult)
+                else:
+                    nc.scalar.activation(out=part, in_=part, func=ACT.Square)
+                nc.sync.dma_start(out=out[n * P : (n + 1) * P, h * 512 + c : h * 512 + c + piece], in_=part)
+
+        quantize_x(1, 0, x1[0][:])
+        pick(6, 512, NJ, 512, "x1_0", 1)
+        shift_into_x1(2, 512, NJ, 512)
+        wave_pass(0, 1)
+        wave_pass(1, 1)
+        line_pass(0, 1)
+        wave_pass(2, 1)
+        line_pass(1, 1)
+        line_pass(2, 1)
+        reduce_angle(0)
+        reduce_angle(1)
+        quantize_x(1, 1, x1[1][:])
+        for u in range(6):
+            ahead = u + 2
+            if ahead < 6:
+                if ahead >= 4:
+                    wave_pass(ahead, 0)
+                if ahead >= 3:
+                    wave_pass(ahead, 1)
+            score(u, 256 if u == 5 else 512)
+            if ahead < 6:
+                reduce_angle(ahead)
+                if ahead >= 4:
+                    line_pass(ahead, 0)
+                if ahead >= 3:
+                    line_pass(ahead, 1)

@@ -22,10 +22,17 @@ P = 128
 PACK = 4
 KP = P * PACK
 QUAD = 32
+QUADS = P // QUAD
+SLICES = H // P
+LAST = SLICES - 1
+HALF = 512
+QUARTER = 256
 TWO_PI = 2.0 * math.pi
 WHOLE = 1.5 * 2.0**23
-SCALAR_TURNS = (2,4,)
-GPSIMD_SQUARES = ()
+UNITS = [(h, n) for h in range(NJ // HALF) for n in range(N // P)]
+UNIT_BANKS = [(0, 1), (2, 3), (4, 5), (6, 7), (0, 2), (4, 6)]
+OPEN_UNITS = 4
+SCALAR_TURNS = range(2, len(UNITS), 2)
 
 
 def tile_list_casing_slot_scores_kernel(
@@ -42,173 +49,195 @@ def tile_list_casing_slot_scores_kernel(
             return sb.tile(shape, dtype, name=name, tag=tag or name, bufs=bufs, align_bytes=64)
 
         def load_list(src, name):
-            t = lists.tile(list(src.shape), U16, name=name)
-            nc.sync.dma_start(t[:], src)
-            return t
+            offsets = lists.tile(list(src.shape), U16, name=name)
+            nc.sync.dma_start(offsets[:], src)
+            return offsets
 
         def load_words(src, name, tag):
-            t = tile([P, src.shape[1]], U32, name, tag)
-            nc.sync.dma_start(out=t[:].bitcast(I32), in_=src.rearrange("p c i -> p (c i)").bitcast(I32))
-            return t
+            words = tile([P, src.shape[1]], U32, name, tag)
+            nc.sync.dma_start(out=words[:].bitcast(I32), in_=src.rearrange("p c i -> p (c i)").bitcast(I32))
+            return words
 
-        def zeroed(width, name, eng):
-            t = tile([P, width], U8, name)
-            eng.memset(t[:].bitcast(I32), 0)
-            return t
+        def zeroed_plane(width, name):
+            plane = tile([P, width], U8, name)
+            nc.vector.memset(plane[:].bitcast(I32), 0)
+            return plane
 
-        def load_scale_rows(plane, src, a=0, quads=range(4)):
+        def load_scale_rows(plane, src, a=0, quads=range(QUADS)):
             for q in quads:
                 first = QUAD * q + 4 * a
                 nc.sync.dma_start(out=plane[first : first + 4, :].bitcast(I32), in_=src[a, 4 * q : 4 * q + 4, :].bitcast(I32))
 
+        def load_float(src, name, tag=None):
+            values = tile(list(src.shape), F32, name, tag)
+            nc.sync.dma_start(out=values[:], in_=src)
+            return values
+
         def load_page(i):
             b, t = divmod(i, PACK)
-            pg = tile([P, T2], F32, "page%d" % i)
-            nc.sync.dma_start(out=pg[:], in_=page0[b * KP : (b + 1) * KP, :].rearrange("(p t) c -> p t c", t=PACK)[:, t, :])
-            return pg
-
-        def load_plain(src, name, tag):
-            t = tile(list(src.shape), F32, name, tag)
-            nc.sync.dma_start(out=t[:], in_=src)
-            return t
+            return load_float(page0[b * KP : (b + 1) * KP, :].rearrange("(p t) c -> p t c", t=PACK)[:, t, :], "page%d" % i)
 
         def load_w1(a, b, tag):
-            return load_plain(w1[a * KP : (a + 1) * KP, b * KP : (b + 1) * KP].rearrange("(p j) c -> p j c", j=PACK), "w1_raw%d%d" % (a, b), tag)
+            block = w1[a * KP : (a + 1) * KP, b * KP : (b + 1) * KP]
+            return load_float(block.rearrange("(p j) c -> p j c", j=PACK), "w1_raw%d%d" % (a, b), tag)
 
         def load_w3(a, tag):
-            return load_plain(w3[a * KP : (a + 1) * KP, :].rearrange("(p j) n -> p j n", j=PACK), "w3_raw%d" % a, tag)
+            return load_float(w3[a * KP : (a + 1) * KP, :].rearrange("(p j) n -> p j n", j=PACK), "w3_raw%d" % a, tag)
 
-        def load_column(src, name):
-            return load_plain(src.rearrange("(b p t) -> p b t", b=2, t=PACK), name, name)
+        def zeroed_rows(name, tag):
+            rows = tile([P, KP], F32, name, tag)
+            nc.gpsimd.memset(rows[:], 0.0)
+            return rows
 
-        banks = [psum.tile([P, 512], F32, name="bank%d" % i) for i in range(8)]
+        def load_rows(rows, src):
+            nc.sync.dma_start(out=rows[0:2, :], in_=src.rearrange("(b c) -> b c", b=2))
 
-        tab2_sc = zeroed(T, "tab2_sc", nc.vector)
-        w2_sc = zeroed(H, "w2_sc", nc.vector)
+        def warm_up(func, after, name, bias=0.0):
+            unused = tile([P, 1], F32, name)
+            nc.scalar.activation(out=unused[:], in_=after[:, 0:1], func=func, scale=0.0, bias=bias)
+
+        banks = [psum.tile([P, HALF], F32, name="bank%d" % i) for i in range(8)]
+
+        gain_rows = zeroed_rows("gain_rows", "v_w1")
         ident = tile([P, P], F32, "ident")
         make_identity(nc, ident[:])
-        tab_sc = zeroed(T, "tab_sc", nc.gpsimd)
-        w4_sc = zeroed(2 * N, "w4_sc", nc.gpsimd)
+        tab2_sc = zeroed_plane(T, "tab2_sc")
+        w2_sc = zeroed_plane(H, "w2_sc")
+        shift_rows = zeroed_rows("shift_rows", "late0")
+        tab_sc = zeroed_plane(T, "tab_sc")
+        w4_sc = zeroed_plane(2 * N, "w4_sc")
+        warm_up(ACT.Tanh, shift_rows, "warm_tanh")
 
         pages, w2_w, tab_w, w1_raw = {}, {}, {}, {}
         idx2 = load_list(offs2, "idx2")
-        gain_sb = load_column(gain, "gain_sb")
-        wg2_rows = load_plain(wg2, "wg2_rows", "x_q00")
+        wg2_rows = load_float(wg2, "wg2_rows", "x_q00")
+        load_rows(gain_rows, gain)
         load_scale_rows(tab2_sc, tab2_scales)
-        tab2_w = load_words(tab2_words[0], "tab2_w", "sA")
+        tab2_w = load_words(tab2_words[0], "tab2_w", "stage_a")
         w2_w[0] = load_words(w2_words[0, :, 0:KP, :], "w2_w0", "w2_w0")
         load_scale_rows(w2_sc, w2_scales)
         pages[0] = load_page(0)
         idx4 = load_list(offs4, "idx4")
-        w2_w[1] = load_words(w2_words[0, :, KP:H, :], "w2_w1", "w2_w1")
         pages[1] = load_page(1)
+        w2_w[1] = load_words(w2_words[0, :, KP:H, :], "w2_w1", "w2_w1")
+        load_rows(shift_rows, shift)
+        wg1_rows = load_float(wg1, "wg1_rows", "x_q01")
         pages[2] = load_page(2)
         load_scale_rows(tab_sc, tab_scales, 0, range(0, 2))
-        wg1_rows = load_plain(wg1, "wg1_rows", "x_q01")
         pages[3] = load_page(3)
         load_scale_rows(tab_sc, tab_scales, 0, range(2, 4))
         idx = load_list(offs, "idx")
-        tab_w[0] = load_words(tab_words[0], "tab_w0", "sB")
+        tab_w[0] = load_words(tab_words[0], "tab_w0", "stage_b")
         load_scale_rows(tab_sc, tab_scales, 1, range(0, 2))
         pages[4] = load_page(4)
         load_scale_rows(tab_sc, tab_scales, 1, range(2, 4))
-        tab_w[1] = load_words(tab_words[1], "tab_w1", "sC")
+        tab_w[1] = load_words(tab_words[1], "tab_w1", "stage_c")
         pages[5] = load_page(5)
-        w1_raw[(0, 0)] = load_w1(0, 0, "sD")
+        w1_raw[(0, 0)] = load_w1(0, 0, "stage_d")
         pages[6] = load_page(6)
-        w1_raw[(1, 0)] = load_w1(1, 0, "sE")
+        w1_raw[(1, 0)] = load_w1(1, 0, "stage_e")
         pages[7] = load_page(7)
         idx3 = load_list(offs3, "idx3")
-        w1_raw[(0, 1)] = load_w1(0, 1, "sF")
+        w1_raw[(0, 1)] = load_w1(0, 1, "stage_f")
 
         v2_w = tile([P, S], U32, "v2_w")
         nc.vector.tensor_copy(out=v2_w[:], in_=tab2_w[:].indirect(idx2[:]))
         v2_sc = tile([P, S], U8, "v2_sc")
         nc.vector.tensor_copy(out=v2_sc[:], in_=tab2_sc[:].indirect(idx2[:]))
 
-        w2_wp = [tile([P, KP], U32, "w2_wp%d" % b) for b in range(2)]
-        w2_scp = [tile([P, KP], U8, "w2_scp%d" % b) for b in range(2)]
+        w2_dealt = [tile([P, KP], U32, "w2_dealt%d" % b) for b in range(2)]
+        w2_sc_dealt = [tile([P, KP], U8, "w2_sc_dealt%d" % b) for b in range(2)]
         for b in range(2):
-            cols = slice(b * KP, (b + 1) * KP)
             nc.vector.tensor_copy(
-                out=w2_wp[b][:].bitcast(I32).rearrange("p (t m) -> p m t", t=PACK),
+                out=w2_dealt[b][:].bitcast(I32).rearrange("p (t m) -> p m t", t=PACK),
                 in_=w2_w[b][:].bitcast(I32).rearrange("p (m t) -> p m t", t=PACK),
             )
             nc.vector.tensor_copy(
-                out=w2_scp[b][:].rearrange("p (t m) -> p m t", t=PACK),
-                in_=w2_sc[:, cols].rearrange("p (m t) -> p m t", t=PACK),
+                out=w2_sc_dealt[b][:].rearrange("p (t m) -> p t m", t=PACK),
+                in_=w2_sc[:, b * KP : (b + 1) * KP].rearrange("p (m t) -> p t m", t=PACK),
             )
 
         def turn(rows, bank):
-            for c in range(4):
+            for c in range(S // P):
                 nc.tensor.transpose(bank[:, c * P : (c + 1) * P], rows[:, c * P : (c + 1) * P], ident[:])
 
         def deal(turned, t, bank, name, tag):
             spread = tile([P, S], F32, name, tag)
+            rows = turned[:].rearrange("j (c m t) -> j c m t", c=S // P, t=PACK)[:, :, :, t]
             nc.scalar.copy(
-                out=spread[:].rearrange("j (c q p) -> j c q p", c=4, q=4),
-                in_=turned[:].rearrange("j (c p t) -> j c p t", c=4, t=PACK)[:, :, :, t].unsqueeze(2).to_broadcast([P, 4, 4, QUAD]),
+                out=spread[:].rearrange("j (c q m) -> j c q m", c=S // P, q=QUADS),
+                in_=rows.unsqueeze(2).to_broadcast([P, S // P, QUADS, QUAD]),
             )
             turn(spread, bank)
 
+        def to_columns(rows, name):
+            for t in range(PACK):
+                nc.tensor.transpose(banks[5][:, t * P : (t + 1) * P], rows[:, t : KP : PACK], ident[:])
+            columns = tile([P, PACK, 2], F32, name)
+            nc.scalar.copy(out=columns[:], in_=banks[5][:].rearrange("p (t b) -> p t b", t=PACK)[:, :, 0:2])
+            return columns
+
+        spread_tags = ("x_q10", "x_q11", "factor0", "factor1")
         turn(wg2_rows, banks[0])
-        wg2g, h2 = {}, {}
-        for i in range(8):
+        gain_cols = to_columns(gain_rows, "gain_cols")
+        h2, factors = {}, {}
+        for i in range(SLICES):
             b, t = divmod(i, PACK)
             if b == 0:
-                deal(banks[0], t, banks[1 + t], "wg2_spread%d" % t, "x_q10" if t == 0 else "w2_sc")
+                deal(banks[0], t, banks[1 + t], "wg2_spread%d" % t, spread_tags[t])
             cols = slice(t * P, (t + 1) * P)
+            product = banks[6 + i % 2]
             nc.tensor.matmul_mx(
-                out=banks[6 + i % 2][:], lhsT=w2_wp[b][:, cols].bitcast(FP8X4), lhsT_scale=w2_scp[b][:, cols],
+                out=product[:], lhsT=w2_dealt[b][:, cols].bitcast(FP8X4), lhsT_scale=w2_sc_dealt[b][:, cols],
                 rhs=v2_w[:].bitcast(FP8X4), rhs_scale=v2_sc[:], start=True, stop=True,
             )
-            wg2g[i] = tile([P, S], F32, "wg2g%d" % i)
-            nc.scalar.activation(out=wg2g[i][:], in_=banks[1 + t][:], func=ACT.Copy, scale=gain_sb[:, b, t : t + 1])
+            factors[i] = tile([P, S], F32, "factor_of%d" % i, "factor%d" % t)
+            nc.scalar.activation(out=factors[i][:], in_=banks[1 + t][:], func=ACT.Copy, scale=gain_cols[:, t, b : b + 1])
             h2[i] = tile([P, S], F32, "h%d" % i)
-            nc.scalar.activation(out=h2[i][:], in_=banks[6 + i % 2][:], func=ACT.Tanh)
-            nc.vector.tensor_tensor(out=pages[i][:].indirect(idx4[:]), in0=h2[i][:], in1=wg2g[i][:], op=ALU.mult)
+            nc.scalar.activation(out=h2[i][:], in_=product[:], func=ACT.Tanh)
+            nc.vector.tensor_tensor(out=pages[i][:].indirect(idx4[:]), in0=h2[i][:], in1=factors[i][:], op=ALU.mult)
 
+        shift_cols = to_columns(shift_rows, "shift_cols")
         turn(wg1_rows, banks[5])
-        wg1_sb = []
+        wg1_dealt = []
         for t in range(PACK):
             deal(banks[5], t, banks[t], "wg1_spread%d" % t, "x_q1%d" % (t % 2))
             dealt = tile([P, S], F32, "wg1_%d" % t)
             nc.scalar.copy(out=dealt[:], in_=banks[t][:])
-            wg1_sb.append(dealt)
+            wg1_dealt.append(dealt)
 
         v_w = []
         for a in range(2):
-            vw = tile([P, S], U32, "v_w%d" % a)
-            nc.vector.tensor_copy(out=vw[:], in_=tab_w[a][:].indirect(idx[:]))
-            v_w.append(vw)
+            picked_words = tile([P, S], U32, "v_w%d" % a)
+            nc.vector.tensor_copy(out=picked_words[:], in_=tab_w[a][:].indirect(idx[:]))
+            v_w.append(picked_words)
         v_sc = tile([P, S], U8, "v_sc")
         nc.vector.tensor_copy(out=v_sc[:], in_=tab_sc[:].indirect(idx[:]))
 
-        w1_raw[(1, 1)] = load_w1(1, 1, "sA")
+        w1_raw[(1, 1)] = load_w1(1, 1, "stage_a")
         idx5 = load_list(offs5, "idx5")
-        shift_sb = load_column(shift, "shift_sb")
-        w3_raw = [load_w3(0, "sB"), load_w3(1, "sC")]
+        w3_raw = [load_w3(0, "stage_b"), load_w3(1, "stage_c")]
         w4_w = tile([P, 2, 2 * N], U8, "w4_w")
         nc.sync.dma_start(out=w4_w[:].bitcast(I32), in_=w4_words.rearrange("a p c -> p a c").bitcast(I32))
-        for q in range(4):
+        for q in range(QUADS):
             nc.sync.dma_start(
                 out=w4_sc[QUAD * q : QUAD * q + 4, :].bitcast(I32).rearrange("p (a n) -> p a n", a=2),
                 in_=w4_scales[:, 4 * q : 4 * q + 4, :].rearrange("a r n -> r a n").bitcast(I32),
             )
 
-        w1_q, w1_s, h1 = {}, {}, {}
+        w1_q, w1_s, sizes, h1 = {}, {}, {}, {}
 
         def quantize_w1(a, b):
-            grouped = tile([P, KP * PACK], BF16, "w1_bf%d%d" % (a, b), "wbf", 2)
+            grouped = tile([P, KP * PACK], BF16, "w1_bf%d%d" % (a, b), "w1_bf", 2)
             nc.scalar.copy(
-                out=grouped[:].rearrange("p (t m j) -> p m j t", t=PACK, j=PACK),
+                out=grouped[:].rearrange("p (t m j) -> p m j t", m=P, j=PACK),
                 in_=w1_raw[(a, b)][:].rearrange("p j (m t) -> p m j t", t=PACK),
             )
             w1_q[(a, b)] = tile([P, KP], U32, "w1_q%d%d" % (a, b))
             w1_s[(a, b)] = tile([P, KP], U8, "w1_s%d%d" % (a, b))
             nc.vector.quantize_mx(out=w1_q[(a, b)][:].bitcast(FP8X4), scales=w1_s[(a, b)][:], in_=grouped[:])
 
-        def make_h1(i):
+        def size_of_h1(i):
             b, t = divmod(i, PACK)
             cols = slice(t * P, (t + 1) * P)
             for a in range(2):
@@ -216,9 +245,12 @@ def tile_list_casing_slot_scores_kernel(
                     out=banks[i][:], lhsT=w1_q[(a, b)][:, cols].bitcast(FP8X4), lhsT_scale=w1_s[(a, b)][:, cols],
                     rhs=v_w[a][:].bitcast(FP8X4), rhs_scale=v_sc[4 * a : P, :], start=(a == 0), stop=(a == 1),
                 )
-            h1[i] = tile([P, S], F32, "h1_%d" % i, "h%d" % (i % 2))
-            nc.scalar.activation(out=h1[i][:], in_=banks[i][:], func=ACT.Abs)
-            nc.scalar.activation(out=h1[i][:], in_=h1[i][:], func=ACT.Sqrt)
+            sizes[i] = tile([P, S], F32, "size%d" % i, "late%d" % (i % 2) if i < LAST else "h1")
+            nc.scalar.activation(out=sizes[i][:], in_=banks[i][:], func=ACT.Abs)
+
+        def root_of_h1(i):
+            h1[i] = tile([P, S], F32, "h1_%d" % i, "h%d" % (i % 2) if i < LAST else "h0")
+            nc.scalar.activation(out=h1[i][:], in_=sizes[i][:], func=ACT.Sqrt)
 
         w3_bf = tile([P, 2 * N * PACK], BF16, "w3_bf")
         w3_q = tile([P, 2 * N], U32, "w3_q")
@@ -231,160 +263,148 @@ def tile_list_casing_slot_scores_kernel(
             )
 
         def quantize_w3():
-            for c0, c1 in ((0, 512), (512, 2 * N)):
+            for c0, c1 in ((0, HALF), (HALF, 2 * N)):
                 nc.vector.quantize_mx(out=w3_q[:, c0:c1].bitcast(FP8X4), scales=w3_s[:, c0:c1], in_=w3_bf[:, PACK * c0 : PACK * c1])
 
-        x_q, x_s = {}, {}
-        units = [(h, n) for h in range(2) for n in range(3)]
-        unit_banks = [(0, 1), (2, 3), (4, 5), (6, 7), (0, 2), (4, 6)]
+        x_q, x_s, picked = {}, {}, {}
 
         def wave_pass(u, b):
-            h, n = units[u]
+            h, n = UNITS[u]
             c0 = b * N + n * P
             nc.tensor.matmul_mx(
-                out=banks[unit_banks[u][0]][:], lhsT=w3_q[:, c0 : c0 + P].bitcast(FP8X4), lhsT_scale=w3_s[:, c0 : c0 + P],
+                out=banks[UNIT_BANKS[u][0]][:], lhsT=w3_q[:, c0 : c0 + P].bitcast(FP8X4), lhsT_scale=w3_s[:, c0 : c0 + P],
                 rhs=x_q[(b, h)][:].bitcast(FP8X4), rhs_scale=x_s[(b, h)][:], start=(b == 0), stop=(b == 1),
             )
 
         def line_pass(u, b):
-            h, n = units[u]
+            h, n = UNITS[u]
             c0 = b * N + n * P
             nc.tensor.matmul_mx(
-                out=banks[unit_banks[u][1]][:], lhsT=w4_w[:, b, 2 * n * P : 2 * (n + 1) * P].bitcast(FP4X4), lhsT_scale=w4_sc[:, c0 : c0 + P],
+                out=banks[UNIT_BANKS[u][1]][:], lhsT=w4_w[:, b, 2 * n * P : 2 * (n + 1) * P].bitcast(FP4X4), lhsT_scale=w4_sc[:, c0 : c0 + P],
                 rhs=x_q[(b, h)][:].bitcast(FP8X4), rhs_scale=x_s[(b, h)][:], start=(b == 0), stop=(b == 1),
             )
 
         def quantize_x(b, h, grouped):
-            x_q[(b, h)] = tile([P, 512], U32, "x_q%d%d" % (b, h))
-            x_s[(b, h)] = tile([P, 512], U8, "x_s%d%d" % (b, h))
+            x_q[(b, h)] = tile([P, HALF], U32, "x_q%d%d" % (b, h))
+            x_s[(b, h)] = tile([P, HALF], U8, "x_s%d%d" % (b, h))
             nc.vector.quantize_mx(out=x_q[(b, h)][:].bitcast(FP8X4), scales=x_s[(b, h)][:], in_=grouped.rearrange("p c t -> p (c t)"))
 
-        picked = {}
+        def piece_of(i):
+            return QUARTER if i == LAST else HALF
 
-        def put(i):
-            nc.vector.tensor_tensor(out=pages[i][:].indirect(idx3[:]), in0=h1[i][:], in1=wg1_sb[i % PACK][:], op=ALU.mult)
+        def put_h1(i):
+            nc.vector.tensor_tensor(out=pages[i][:].indirect(idx3[:]), in0=h1[i][:], in1=wg1_dealt[i % PACK][:], op=ALU.mult)
 
-        def pick(i, c0, c1, piece, tag="picked", bufs=2):
-            picked[(i, c0)] = tile([P, c1 - c0], F32, "picked%d_%d" % (i, c0), tag, bufs)
-            for c in range(c0, c1, piece):
-                nc.vector.tensor_copy(out=picked[(i, c0)][:, c - c0 : c - c0 + piece], in_=pages[i][:].indirect(idx5[:, c // 16 : (c + piece) // 16]))
+        def pick(i, h, tag="picked", bufs=2):
+            picked[(i, h)] = tile([P, HALF], F32, "picked%d_%d" % (i, h), tag, bufs)
+            for c in range(0, HALF, piece_of(i)):
+                entries = idx5[:, (h * HALF + c) // 16 : (h * HALF + c + piece_of(i)) // 16]
+                nc.vector.tensor_copy(out=picked[(i, h)][:, c : c + piece_of(i)], in_=pages[i][:].indirect(entries))
 
-        x_planes = tile([P, PACK, NJ], BF16, "x_planes", "sD")
-        x0 = tile([P, NJ, PACK], BF16, "x0", "sE")
-        x1 = [tile([P, 512, PACK], BF16, "x1_%d" % h) for h in range(2)]
+        x0_apart = tile([P, PACK, NJ], BF16, "x0_apart", "stage_d")
+        x0 = tile([P, NJ, PACK], BF16, "x0", "stage_e")
+        x1 = [tile([P, HALF, PACK], BF16, "x1_%d" % h) for h in range(2)]
 
-        def shift_plane(t):
-            nc.scalar.activation(out=x_planes[:, t, :], in_=picked[(t, 0)][:], func=ACT.Identity, bias=shift_sb[:, 0, t : t + 1])
+        def add_shift(i, h):
+            b, t = divmod(i, PACK)
+            for c in range(0, HALF, piece_of(i)):
+                cols = slice(c, c + piece_of(i))
+                target = x0_apart[:, t, h * HALF : (h + 1) * HALF] if b == 0 else x1[h][:, cols, t]
+                nc.scalar.activation(out=target, in_=picked[(i, h)][:, cols], func=ACT.Identity, bias=shift_cols[:, t, b : b + 1])
 
         def weave_x0(h):
-            cols = slice(h * 512, (h + 1) * 512)
+            cols = slice(h * HALF, (h + 1) * HALF)
             nc.scalar.copy(
                 out=x0[:, cols, :].rearrange("p (c i) t -> p c t i", i=4),
-                in_=x_planes[:, :, cols].rearrange("p t (c i) -> p c t i", i=4),
+                in_=x0_apart[:, :, cols].rearrange("p t (c i) -> p c t i", i=4),
             )
             quantize_x(0, h, x0[:, cols, :])
 
-        def shift_into_x1(t, c0, c1, piece):
-            for c in range(c0, c1, piece):
-                h, col = divmod(c, 512)
-                nc.scalar.activation(
-                    out=x1[h][:, col : col + piece, t], in_=picked[(PACK + t, c0)][:, c - c0 : c - c0 + piece],
-                    func=ACT.Identity, bias=shift_sb[:, 1, t : t + 1],
-                )
-
-        warm_sqrt = tile([P, 1], F32, "warm_sqrt")
-        nc.scalar.activation(out=warm_sqrt[:], in_=h2[7][:, 0:1], func=ACT.Sqrt, scale=0.0, bias=1.0)
-        quantize_w1(0, 0)
-        quantize_w1(1, 0)
-        quantize_w1(0, 1)
-        quantize_w1(1, 1)
-        make_h1(0)
-        make_h1(1)
-        for i in range(8):
-            width = 512 if i == 6 else NJ
-            put(i)
-            if i < 7:
-                pick(i, 0, width, width)
-            else:
-                pick(i, 0, 512, 256)
-                pick(i, 512, NJ, 256)
-            if i + 2 < 8:
-                make_h1(i + 2)
-            if i == 5:
-                warm_sin = tile([P, 1], F32, "warm_sin")
-                nc.scalar.activation(out=warm_sin[:], in_=h1[7][:, 0:1], func=ACT.Sin, scale=0.0)
-            if i == 1:
-                round_w3(0)
+        warm_up(ACT.Sqrt, factors[LAST], "warm_sqrt", bias=1.0)
+        for b in range(2):
+            for a in range(2):
+                quantize_w1(a, b)
+        for i in range(2):
+            size_of_h1(i)
+            root_of_h1(i)
+        for i in range(SLICES):
+            put_h1(i)
+            if i == LAST - 1:
+                root_of_h1(LAST)
+            late = 1 <= i < LAST
+            if late:
+                pick(i - 1, 1, "late%d" % (i % 2), 1)
+            pick(i, 0)
+            if i == LAST:
+                pick(i, 1)
+            if late:
+                add_shift(i - 1, 1)
+            if i + 2 <= LAST:
+                size_of_h1(i + 2)
+            if i + 2 < LAST:
+                root_of_h1(i + 2)
+            if i == LAST - 1:
+                warm_up(ACT.Sin, h1[LAST], "warm_sin")
+            if i in (1, 2):
+                round_w3(i - 1)
             if i == 2:
-                round_w3(1)
                 quantize_w3()
-            if i < 4:
-                shift_plane(i)
-            else:
-                if i < 7:
-                    shift_into_x1(i - 4, 0, width, 512)
-                else:
-                    shift_into_x1(3, 0, 512, 256)
-                    shift_into_x1(3, 512, NJ, 256)
-            if i in (3, 4):
-                weave_x0(i - 3)
-            if i == 5:
-                for u in range(4):
+            add_shift(i, 0)
+            if i == LAST:
+                add_shift(i, 1)
+            if i in (PACK - 1, PACK):
+                weave_x0(i - PACK + 1)
+            if i == LAST - 2:
+                for u in range(OPEN_UNITS):
                     wave_pass(u, 0)
                     line_pass(u, 0)
 
-        angles, diffs = {}, {}
+        angles = {}
+        diff_tags = ("stage_a", "stage_b", "stage_c", "stage_f", "w3_bf", "v_w0")
 
-        def reduce_angle(u):
-            bank_a = banks[unit_banks[u][0]]
-            tag = "h%d" % (u + 2)
+        def sine(u):
+            argument = banks[UNIT_BANKS[u][0]]
             if u in SCALAR_TURNS:
-                biased = tile([P, 512], U32, "biased%d" % u, "wg1_%d" % (u % 4))
-                nc.scalar.activation(out=biased[:], in_=bank_a[:], func=ACT.Copy, scale=1.0 / TWO_PI, bias=WHOLE)
-                turns = tile([P, 512], F32, "turns%d" % u, tag)
+                biased = tile([P, HALF], U32, "biased%d" % u, "wg1_%d" % (u % PACK))
+                nc.scalar.activation(out=biased[:], in_=argument[:], func=ACT.Copy, scale=1.0 / TWO_PI, bias=WHOLE)
+                turns = tile([P, HALF], F32, "turns%d" % u, "h%d" % (u + 2))
                 nc.scalar.activation(out=turns[:], in_=biased[:], func=ACT.Copy, bias=-WHOLE)
             else:
-                turns = tile([P, 512], I32, "turns%d" % u, tag)
-                nc.vector.tensor_scalar(out=turns[:], in0=bank_a[:], scalar1=1.0 / TWO_PI, scalar2=None, op0=ALU.mult)
-            angles[u] = tile([P, 512], F32, "angle%d" % u, "wg2g%d" % u)
-            nc.vector.scalar_tensor_tensor(out=angles[u][:], in0=turns[:], scalar=-TWO_PI, in1=bank_a[:], op0=ALU.mult, op1=ALU.add)
+                turns = tile([P, HALF], I32, "turns%d" % u, "h%d" % (u + 2))
+                nc.vector.tensor_scalar(out=turns[:], in0=argument[:], scalar1=1.0 / TWO_PI, scalar2=None, op0=ALU.mult)
+            angles[u] = tile([P, HALF], F32, "angle%d" % u, "factor%d" % u if u < PACK else "late%d" % (u - PACK))
+            nc.vector.scalar_tensor_tensor(out=angles[u][:], in0=turns[:], scalar=-TWO_PI, in1=argument[:], op0=ALU.mult, op1=ALU.add)
             nc.scalar.activation(out=angles[u][:], in_=angles[u][:], func=ACT.Sin)
 
-        def score(u, piece):
-            h, n = units[u]
-            diffs[u] = tile([P, 512], F32, "diff%d" % u, ("sA", "sB", "sC", "sF", "w3_bf", "v_w0")[u])
-            for c in range(0, 512, piece):
-                part = diffs[u][:, c : c + piece]
-                nc.vector.tensor_tensor(out=part, in0=banks[unit_banks[u][1]][:, c : c + piece], in1=angles[u][:, c : c + piece], op=ALU.subtract)
-                if u in GPSIMD_SQUARES:
-                    nc.gpsimd.tensor_tensor(out=part, in0=part, in1=part, op=ALU.mult)
-                else:
-                    nc.scalar.activation(out=part, in_=part, func=ACT.Square)
-                nc.sync.dma_start(out=out[n * P : (n + 1) * P, h * 512 + c : h * 512 + c + piece], in_=part)
+        def score(u):
+            h, n = UNITS[u]
+            piece = QUARTER if u == len(UNITS) - 1 else HALF
+            diff = tile([P, HALF], F32, "diff%d" % u, diff_tags[u])
+            for c in range(0, HALF, piece):
+                part = diff[:, c : c + piece]
+                nc.vector.tensor_tensor(out=part, in0=banks[UNIT_BANKS[u][1]][:, c : c + piece], in1=angles[u][:, c : c + piece], op=ALU.subtract)
+                nc.scalar.activation(out=part, in_=part, func=ACT.Square)
+                nc.sync.dma_start(out=out[n * P : (n + 1) * P, h * HALF + c : h * HALF + c + piece], in_=part)
 
         quantize_x(1, 0, x1[0][:])
-        pick(6, 512, NJ, 512, "x1_0", 1)
-        shift_into_x1(2, 512, NJ, 512)
+        pick(LAST - 1, 1, "x1_0", 1)
+        add_shift(LAST - 1, 1)
+        first_half = N // P
         wave_pass(0, 1)
-        wave_pass(1, 1)
-        line_pass(0, 1)
-        wave_pass(2, 1)
-        line_pass(1, 1)
-        line_pass(2, 1)
-        reduce_angle(0)
-        reduce_angle(1)
+        for u in range(first_half):
+            if u + 1 < first_half:
+                wave_pass(u + 1, 1)
+            line_pass(u, 1)
+        sine(0)
+        sine(1)
         quantize_x(1, 1, x1[1][:])
-        for u in range(6):
+        for u in range(len(UNITS)):
             ahead = u + 2
-            if ahead < 6:
-                if ahead >= 4:
-                    wave_pass(ahead, 0)
-                if ahead >= 3:
-                    wave_pass(ahead, 1)
-            score(u, 256 if u == 5 else 512)
-            if ahead < 6:
-                reduce_angle(ahead)
-                if ahead >= 4:
-                    line_pass(ahead, 0)
-                if ahead >= 3:
-                    line_pass(ahead, 1)
+            passes = [b for b in range(2) if first_half <= ahead < len(UNITS) and (b == 1 or ahead >= OPEN_UNITS)]
+            for b in passes:
+                wave_pass(ahead, b)
+            score(u)
+            if ahead < len(UNITS):
+                sine(ahead)
+            for b in passes:
+                line_pass(ahead, b)

import math
from contextlib import ExitStack

import concourse.mybir as mybir
from concourse.masks import make_identity

K, K2, T, S, H, T2, NJ, N = 1024, 512, 2048, 512, 1024, 2048, 1024, 384
FLOPS = 2 * (K * H * S + K2 * H * S + 2 * H * N * NJ)

F32 = mybir.dt.float32
BF16 = mybir.dt.bfloat16
I32 = mybir.dt.int32
U32 = mybir.dt.uint32
U16 = mybir.dt.uint16
U8 = mybir.dt.uint8
FP8X4 = mybir.dt.float8_e4m3fn_x4
FP4X4 = mybir.dt.float4_e2m1fn_x4
ALU = mybir.AluOpType
ACT = mybir.ActivationFunctionType

P = 128
PACK = 4
KP = P * PACK
QUAD = 32
QUADS = P // QUAD
SLICES = H // P
LAST = SLICES - 1
HALF = 512
QUARTER = 256
TWO_PI = 2.0 * math.pi
WHOLE = 1.5 * 2.0**23
UNITS = [(h, n) for h in range(NJ // HALF) for n in range(N // P)]
UNIT_BANKS = [(0, 1), (2, 3), (4, 5), (6, 7), (0, 2), (4, 6)]
OPEN_UNITS = 4
SCALAR_TURNS = range(2, len(UNITS), 2)


def tile_list_casing_slot_scores_kernel(
    tc, tab_words, tab_scales, tab2_words, tab2_scales, offs, offs2, offs3, offs4, offs5,
    w1, w2_words, w2_scales, gain, page0, wg1, wg2, shift, w3, w4_words, w4_scales, out,
):
    nc = tc.nc
    with ExitStack() as ctx:
        lists = ctx.enter_context(tc.tile_pool(name="lists", bufs=1))
        sb = ctx.enter_context(tc.tile_pool(name="sb", bufs=1))
        psum = ctx.enter_context(tc.psum_pool(name="psum", bufs=1))

        def tile(shape, dtype, name, tag=None, bufs=1):
            return sb.tile(shape, dtype, name=name, tag=tag or name, bufs=bufs, align_bytes=64)

        def load_list(src, name):
            offsets = lists.tile(list(src.shape), U16, name=name)
            nc.sync.dma_start(offsets[:], src)
            return offsets

        def load_words(src, name, tag):
            words = tile([P, src.shape[1]], U32, name, tag)
            nc.sync.dma_start(out=words[:].bitcast(I32), in_=src.rearrange("p c i -> p (c i)").bitcast(I32))
            return words

        def zeroed_plane(width, name):
            plane = tile([P, width], U8, name)
            nc.vector.memset(plane[:].bitcast(I32), 0)
            return plane

        def load_scale_rows(plane, src, a=0, quads=range(QUADS)):
            for q in quads:
                first = QUAD * q + 4 * a
                nc.sync.dma_start(out=plane[first : first + 4, :].bitcast(I32), in_=src[a, 4 * q : 4 * q + 4, :].bitcast(I32))

        def load_float(src, name, tag=None):
            values = tile(list(src.shape), F32, name, tag)
            nc.sync.dma_start(out=values[:], in_=src)
            return values

        def load_page(i):
            b, t = divmod(i, PACK)
            return load_float(page0[b * KP : (b + 1) * KP, :].rearrange("(p t) c -> p t c", t=PACK)[:, t, :], "page%d" % i)

        def load_w1(a, b, tag):
            block = w1[a * KP : (a + 1) * KP, b * KP : (b + 1) * KP]
            return load_float(block.rearrange("(p j) c -> p j c", j=PACK), "w1_raw%d%d" % (a, b), tag)

        def load_w3(a, tag):
            return load_float(w3[a * KP : (a + 1) * KP, :].rearrange("(p j) n -> p j n", j=PACK), "w3_raw%d" % a, tag)

        def zeroed_rows(name, tag):
            rows = tile([P, KP], F32, name, tag)
            nc.gpsimd.memset(rows[:], 0.0)
            return rows

        def load_rows(rows, src):
            nc.sync.dma_start(out=rows[0:2, :], in_=src.rearrange("(b c) -> b c", b=2))

        def warm_up(func, after, name, bias=0.0):
            unused = tile([P, 1], F32, name)
            nc.scalar.activation(out=unused[:], in_=after[:, 0:1], func=func, scale=0.0, bias=bias)

        banks = [psum.tile([P, HALF], F32, name="bank%d" % i) for i in range(8)]

        gain_rows = zeroed_rows("gain_rows", "v_w1")
        ident = tile([P, P], F32, "ident")
        make_identity(nc, ident[:])
        tab2_sc = zeroed_plane(T, "tab2_sc")
        w2_sc = zeroed_plane(H, "w2_sc")
        shift_rows = zeroed_rows("shift_rows", "late0")
        tab_sc = zeroed_plane(T, "tab_sc")
        w4_sc = zeroed_plane(2 * N, "w4_sc")
        warm_up(ACT.Tanh, shift_rows, "warm_tanh")

        pages, w2_w, tab_w, w1_raw = {}, {}, {}, {}
        idx2 = load_list(offs2, "idx2")
        wg2_rows = load_float(wg2, "wg2_rows", "x_q00")
        load_rows(gain_rows, gain)
        load_scale_rows(tab2_sc, tab2_scales)
        tab2_w = load_words(tab2_words[0], "tab2_w", "stage_a")
        w2_w[0] = load_words(w2_words[0, :, 0:KP, :], "w2_w0", "w2_w0")
        load_scale_rows(w2_sc, w2_scales)
        pages[0] = load_page(0)
        idx4 = load_list(offs4, "idx4")
        pages[1] = load_page(1)
        w2_w[1] = load_words(w2_words[0, :, KP:H, :], "w2_w1", "w2_w1")
        load_rows(shift_rows, shift)
        wg1_rows = load_float(wg1, "wg1_rows", "x_q01")
        pages[2] = load_page(2)
        load_scale_rows(tab_sc, tab_scales, 0, range(0, 2))
        pages[3] = load_page(3)
        load_scale_rows(tab_sc, tab_scales, 0, range(2, 4))
        idx = load_list(offs, "idx")
        tab_w[0] = load_words(tab_words[0], "tab_w0", "stage_b")
        load_scale_rows(tab_sc, tab_scales, 1, range(0, 2))
        pages[4] = load_page(4)
        load_scale_rows(tab_sc, tab_scales, 1, range(2, 4))
        tab_w[1] = load_words(tab_words[1], "tab_w1", "stage_c")
        pages[5] = load_page(5)
        w1_raw[(0, 0)] = load_w1(0, 0, "stage_d")
        pages[6] = load_page(6)
        w1_raw[(1, 0)] = load_w1(1, 0, "stage_e")
        pages[7] = load_page(7)
        idx3 = load_list(offs3, "idx3")
        w1_raw[(0, 1)] = load_w1(0, 1, "stage_f")

        v2_w = tile([P, S], U32, "v2_w")
        nc.vector.tensor_copy(out=v2_w[:], in_=tab2_w[:].indirect(idx2[:]))
        v2_sc = tile([P, S], U8, "v2_sc")
        nc.vector.tensor_copy(out=v2_sc[:], in_=tab2_sc[:].indirect(idx2[:]))

        w2_dealt = [tile([P, KP], U32, "w2_dealt%d" % b) for b in range(2)]
        w2_sc_dealt = [tile([P, KP], U8, "w2_sc_dealt%d" % b) for b in range(2)]
        for b in range(2):
            nc.vector.tensor_copy(
                out=w2_dealt[b][:].bitcast(I32).rearrange("p (t m) -> p m t", t=PACK),
                in_=w2_w[b][:].bitcast(I32).rearrange("p (m t) -> p m t", t=PACK),
            )
            nc.vector.tensor_copy(
                out=w2_sc_dealt[b][:].rearrange("p (t m) -> p t m", t=PACK),
                in_=w2_sc[:, b * KP : (b + 1) * KP].rearrange("p (m t) -> p t m", t=PACK),
            )

        def turn(rows, bank):
            for c in range(S // P):
                nc.tensor.transpose(bank[:, c * P : (c + 1) * P], rows[:, c * P : (c + 1) * P], ident[:])

        def deal(turned, t, bank, name, tag):
            spread = tile([P, S], F32, name, tag)
            rows = turned[:].rearrange("j (c m t) -> j c m t", c=S // P, t=PACK)[:, :, :, t]
            nc.scalar.copy(
                out=spread[:].rearrange("j (c q m) -> j c q m", c=S // P, q=QUADS),
                in_=rows.unsqueeze(2).to_broadcast([P, S // P, QUADS, QUAD]),
            )
            turn(spread, bank)

        def to_columns(rows, name):
            for t in range(PACK):
                nc.tensor.transpose(banks[5][:, t * P : (t + 1) * P], rows[:, t : KP : PACK], ident[:])
            columns = tile([P, PACK, 2], F32, name)
            nc.scalar.copy(out=columns[:], in_=banks[5][:].rearrange("p (t b) -> p t b", t=PACK)[:, :, 0:2])
            return columns

        spread_tags = ("x_q10", "x_q11", "factor0", "factor1")
        turn(wg2_rows, banks[0])
        gain_cols = to_columns(gain_rows, "gain_cols")
        h2, factors = {}, {}
        for i in range(SLICES):
            b, t = divmod(i, PACK)
            if b == 0:
                deal(banks[0], t, banks[1 + t], "wg2_spread%d" % t, spread_tags[t])
            cols = slice(t * P, (t + 1) * P)
            product = banks[6 + i % 2]
            nc.tensor.matmul_mx(
                out=product[:], lhsT=w2_dealt[b][:, cols].bitcast(FP8X4), lhsT_scale=w2_sc_dealt[b][:, cols],
                rhs=v2_w[:].bitcast(FP8X4), rhs_scale=v2_sc[:], start=True, stop=True,
            )
            factors[i] = tile([P, S], F32, "factor_of%d" % i, "factor%d" % t)
            nc.scalar.activation(out=factors[i][:], in_=banks[1 + t][:], func=ACT.Copy, scale=gain_cols[:, t, b : b + 1])
            h2[i] = tile([P, S], F32, "h%d" % i)
            nc.scalar.activation(out=h2[i][:], in_=product[:], func=ACT.Tanh)
            nc.vector.tensor_tensor(out=pages[i][:].indirect(idx4[:]), in0=h2[i][:], in1=factors[i][:], op=ALU.mult)

        shift_cols = to_columns(shift_rows, "shift_cols")
        turn(wg1_rows, banks[5])
        wg1_dealt = []
        for t in range(PACK):
            deal(banks[5], t, banks[t], "wg1_spread%d" % t, "x_q1%d" % (t % 2))
            dealt = tile([P, S], F32, "wg1_%d" % t)
            nc.scalar.copy(out=dealt[:], in_=banks[t][:])
            wg1_dealt.append(dealt)

        v_w = []
        for a in range(2):
            picked_words = tile([P, S], U32, "v_w%d" % a)
            nc.vector.tensor_copy(out=picked_words[:], in_=tab_w[a][:].indirect(idx[:]))
            v_w.append(picked_words)
        v_sc = tile([P, S], U8, "v_sc")
        nc.vector.tensor_copy(out=v_sc[:], in_=tab_sc[:].indirect(idx[:]))

        w1_raw[(1, 1)] = load_w1(1, 1, "stage_a")
        idx5 = load_list(offs5, "idx5")
        w3_raw = [load_w3(0, "stage_b"), load_w3(1, "stage_c")]
        w4_w = tile([P, 2, 2 * N], U8, "w4_w")
        nc.sync.dma_start(out=w4_w[:].bitcast(I32), in_=w4_words.rearrange("a p c -> p a c").bitcast(I32))
        for q in range(QUADS):
            nc.sync.dma_start(
                out=w4_sc[QUAD * q : QUAD * q + 4, :].bitcast(I32).rearrange("p (a n) -> p a n", a=2),
                in_=w4_scales[:, 4 * q : 4 * q + 4, :].rearrange("a r n -> r a n").bitcast(I32),
            )

        w1_q, w1_s, sizes, h1 = {}, {}, {}, {}

        def quantize_w1(a, b):
            grouped = tile([P, KP * PACK], BF16, "w1_bf%d%d" % (a, b), "w1_bf", 2)
            nc.scalar.copy(
                out=grouped[:].rearrange("p (t m j) -> p m j t", m=P, j=PACK),
                in_=w1_raw[(a, b)][:].rearrange("p j (m t) -> p m j t", t=PACK),
            )
            w1_q[(a, b)] = tile([P, KP], U32, "w1_q%d%d" % (a, b))
            w1_s[(a, b)] = tile([P, KP], U8, "w1_s%d%d" % (a, b))
            nc.vector.quantize_mx(out=w1_q[(a, b)][:].bitcast(FP8X4), scales=w1_s[(a, b)][:], in_=grouped[:])

        def size_of_h1(i):
            b, t = divmod(i, PACK)
            cols = slice(t * P, (t + 1) * P)
            for a in range(2):
                nc.tensor.matmul_mx(
                    out=banks[i][:], lhsT=w1_q[(a, b)][:, cols].bitcast(FP8X4), lhsT_scale=w1_s[(a, b)][:, cols],
                    rhs=v_w[a][:].bitcast(FP8X4), rhs_scale=v_sc[4 * a : P, :], start=(a == 0), stop=(a == 1),
                )
            sizes[i] = tile([P, S], F32, "size%d" % i, "late%d" % (i % 2) if i < LAST else "h1")
            nc.scalar.activation(out=sizes[i][:], in_=banks[i][:], func=ACT.Abs)

        def root_of_h1(i):
            h1[i] = tile([P, S], F32, "h1_%d" % i, "h%d" % (i % 2) if i < LAST else "h0")
            nc.scalar.activation(out=h1[i][:], in_=sizes[i][:], func=ACT.Sqrt)

        w3_bf = tile([P, 2 * N * PACK], BF16, "w3_bf")
        w3_q = tile([P, 2 * N], U32, "w3_q")
        w3_s = tile([P, 2 * N], U8, "w3_s")

        def round_w3(a):
            nc.scalar.copy(
                out=w3_bf[:, a * N * PACK : (a + 1) * N * PACK].rearrange("p (c i j) -> p c j i", i=4, j=PACK),
                in_=w3_raw[a][:].rearrange("p j (c i) -> p c j i", i=4),
            )

        def quantize_w3():
            for c0, c1 in ((0, HALF), (HALF, 2 * N)):
                nc.vector.quantize_mx(out=w3_q[:, c0:c1].bitcast(FP8X4), scales=w3_s[:, c0:c1], in_=w3_bf[:, PACK * c0 : PACK * c1])

        x_q, x_s, picked = {}, {}, {}

        def wave_pass(u, b):
            h, n = UNITS[u]
            c0 = b * N + n * P
            nc.tensor.matmul_mx(
                out=banks[UNIT_BANKS[u][0]][:], lhsT=w3_q[:, c0 : c0 + P].bitcast(FP8X4), lhsT_scale=w3_s[:, c0 : c0 + P],
                rhs=x_q[(b, h)][:].bitcast(FP8X4), rhs_scale=x_s[(b, h)][:], start=(b == 0), stop=(b == 1),
            )

        def line_pass(u, b):
            h, n = UNITS[u]
            c0 = b * N + n * P
            nc.tensor.matmul_mx(
                out=banks[UNIT_BANKS[u][1]][:], lhsT=w4_w[:, b, 2 * n * P : 2 * (n + 1) * P].bitcast(FP4X4), lhsT_scale=w4_sc[:, c0 : c0 + P],
                rhs=x_q[(b, h)][:].bitcast(FP8X4), rhs_scale=x_s[(b, h)][:], start=(b == 0), stop=(b == 1),
            )

        def quantize_x(b, h, grouped):
            x_q[(b, h)] = tile([P, HALF], U32, "x_q%d%d" % (b, h))
            x_s[(b, h)] = tile([P, HALF], U8, "x_s%d%d" % (b, h))
            nc.vector.quantize_mx(out=x_q[(b, h)][:].bitcast(FP8X4), scales=x_s[(b, h)][:], in_=grouped.rearrange("p c t -> p (c t)"))

        def piece_of(i):
            return QUARTER if i == LAST else HALF

        def put_h1(i):
            nc.vector.tensor_tensor(out=pages[i][:].indirect(idx3[:]), in0=h1[i][:], in1=wg1_dealt[i % PACK][:], op=ALU.mult)

        def pick(i, h, tag="picked", bufs=2):
            picked[(i, h)] = tile([P, HALF], F32, "picked%d_%d" % (i, h), tag, bufs)
            for c in range(0, HALF, piece_of(i)):
                entries = idx5[:, (h * HALF + c) // 16 : (h * HALF + c + piece_of(i)) // 16]
                nc.vector.tensor_copy(out=picked[(i, h)][:, c : c + piece_of(i)], in_=pages[i][:].indirect(entries))

        x0_apart = tile([P, PACK, NJ], BF16, "x0_apart", "stage_d")
        x0 = tile([P, NJ, PACK], BF16, "x0", "stage_e")
        x1 = [tile([P, HALF, PACK], BF16, "x1_%d" % h) for h in range(2)]

        def add_shift(i, h):
            b, t = divmod(i, PACK)
            for c in range(0, HALF, piece_of(i)):
                cols = slice(c, c + piece_of(i))
                target = x0_apart[:, t, h * HALF : (h + 1) * HALF] if b == 0 else x1[h][:, cols, t]
                nc.scalar.activation(out=target, in_=picked[(i, h)][:, cols], func=ACT.Identity, bias=shift_cols[:, t, b : b + 1])

        def weave_x0(h):
            cols = slice(h * HALF, (h + 1) * HALF)
            nc.scalar.copy(
                out=x0[:, cols, :].rearrange("p (c i) t -> p c t i", i=4),
                in_=x0_apart[:, :, cols].rearrange("p t (c i) -> p c t i", i=4),
            )
            quantize_x(0, h, x0[:, cols, :])

        warm_up(ACT.Sqrt, factors[LAST], "warm_sqrt", bias=1.0)
        for b in range(2):
            for a in range(2):
                quantize_w1(a, b)
        for i in range(2):
            size_of_h1(i)
            root_of_h1(i)
        for i in range(SLICES):
            put_h1(i)
            if i == LAST - 1:
                root_of_h1(LAST)
            late = 1 <= i < LAST
            if late:
                pick(i - 1, 1, "late%d" % (i % 2), 1)
            pick(i, 0)
            if i == LAST:
                pick(i, 1)
            if late:
                add_shift(i - 1, 1)
            if i + 2 <= LAST:
                size_of_h1(i + 2)
            if i + 2 < LAST:
                root_of_h1(i + 2)
            if i == LAST - 1:
                warm_up(ACT.Sin, h1[LAST], "warm_sin")
            if i in (1, 2):
                round_w3(i - 1)
            if i == 2:
                quantize_w3()
            add_shift(i, 0)
            if i == LAST:
                add_shift(i, 1)
            if i in (PACK - 1, PACK):
                weave_x0(i - PACK + 1)
            if i == LAST - 2:
                for u in range(OPEN_UNITS):
                    wave_pass(u, 0)
                    line_pass(u, 0)

        angles = {}
        diff_tags = ("stage_a", "stage_b", "stage_c", "stage_f", "w3_bf", "v_w0")

        def sine(u):
            argument = banks[UNIT_BANKS[u][0]]
            if u in SCALAR_TURNS:
                biased = tile([P, HALF], U32, "biased%d" % u, "wg1_%d" % (u % PACK))
                nc.scalar.activation(out=biased[:], in_=argument[:], func=ACT.Copy, scale=1.0 / TWO_PI, bias=WHOLE)
                turns = tile([P, HALF], F32, "turns%d" % u, "h%d" % (u + 2))
                nc.scalar.activation(out=turns[:], in_=biased[:], func=ACT.Copy, bias=-WHOLE)
            else:
                turns = tile([P, HALF], I32, "turns%d" % u, "h%d" % (u + 2))
                nc.vector.tensor_scalar(out=turns[:], in0=argument[:], scalar1=1.0 / TWO_PI, scalar2=None, op0=ALU.mult)
            angles[u] = tile([P, HALF], F32, "angle%d" % u, "factor%d" % u if u < PACK else "late%d" % (u - PACK))
            nc.vector.scalar_tensor_tensor(out=angles[u][:], in0=turns[:], scalar=-TWO_PI, in1=argument[:], op0=ALU.mult, op1=ALU.add)
            nc.scalar.activation(out=angles[u][:], in_=angles[u][:], func=ACT.Sin)

        def score(u):
            h, n = UNITS[u]
            piece = QUARTER if u == len(UNITS) - 1 else HALF
            diff = tile([P, HALF], F32, "diff%d" % u, diff_tags[u])
            for c in range(0, HALF, piece):
                part = diff[:, c : c + piece]
                nc.vector.tensor_tensor(out=part, in0=banks[UNIT_BANKS[u][1]][:, c : c + piece], in1=angles[u][:, c : c + piece], op=ALU.subtract)
                nc.scalar.activation(out=part, in_=part, func=ACT.Square)
                nc.sync.dma_start(out=out[n * P : (n + 1) * P, h * HALF + c : h * HALF + c + piece], in_=part)

        quantize_x(1, 0, x1[0][:])
        pick(LAST - 1, 1, "x1_0", 1)
        add_shift(LAST - 1, 1)
        first_half = N // P
        wave_pass(0, 1)
        for u in range(first_half):
            if u + 1 < first_half:
                wave_pass(u + 1, 1)
            line_pass(u, 1)
        sine(0)
        sine(1)
        quantize_x(1, 1, x1[1][:])
        for u in range(len(UNITS)):
            ahead = u + 2
            passes = [b for b in range(2) if first_half <= ahead < len(UNITS) and (b == 1 or ahead >= OPEN_UNITS)]
            for b in passes:
                wave_pass(ahead, b)
            score(u)
            if ahead < len(UNITS):
                sine(ahead)
            for b in passes:
                line_pass(ahead, b)
